import numpy as np
import ml_dtypes


def mxq(x, axis, fmt="e4m3"):
    dtype, down = {"e4m3": (ml_dtypes.float8_e4m3fn, 7), "e5m2": (ml_dtypes.float8_e5m2, 14)}[fmt]
    v = np.moveaxis(np.asarray(x, np.float32).astype(ml_dtypes.bfloat16).astype(np.float64), axis, -1)
    blocks = v.reshape(v.shape[:-1] + (-1, 32))
    amax = np.abs(blocks).max(-1, keepdims=True)
    byte = np.maximum(np.where(amax > 0, np.frexp(amax)[1] - 1 + 127, 0) - down, 1)
    scale = np.exp2(byte - 127.0)
    codes = (blocks / scale).astype(np.float32).astype(dtype).astype(np.float64)
    return np.moveaxis((codes * scale).reshape(v.shape), -1, axis)


WIDE = False


def mx_kscale(k):
    if not WIDE:
        return np.ones(k)
    levels = np.array([10, -10, 5, -5, 0])
    if k % 512:
        return np.exp2(np.random.permutation(np.resize(levels, k // 32))).repeat(32)
    a = np.empty((k // 512, 16))
    for p in range(k // 512):
        a[p, :8] = np.random.permutation(np.resize(levels, 8))
        for g in range(8):
            far = levels[np.abs(levels - a[p, g]) >= 10]
            a[p, g + 8] = far[np.random.randint(len(far))]
    return np.exp2(a.ravel()).repeat(32)


def f64(x):
    return np.asarray(x).astype(np.float64)


def striped(idx):
    return np.tile(idx.reshape(-1, 16).T, (8, 1)).astype(np.uint16)


def unstriped(offs):
    return offs[:16].T.reshape(-1).astype(np.int64)


E2M1 = np.array([0.0, 0.5, 1.0, 1.5, 2.0, 3.0, 4.0, 6.0, -0.0, -0.5, -1.0, -1.5, -2.0, -3.0, -4.0, -6.0])


def pack_weight(w, fmt):
    k, n = w.shape
    w = f64(np.asarray(w, np.float32).astype(ml_dtypes.bfloat16)).reshape(k // 32, 32, n)
    amax = np.abs(w).max(1)
    if fmt == "e4m3":
        byte = np.frexp(amax)[1] - 1 + 127 - 7
    else:
        mant, ex = np.frexp(amax / 6.0)
        byte = np.where(mant > 0.5, ex, ex - 1) + 127
    byte = np.clip(np.where(amax > 0, byte, 1), 1, 254)
    scaled = (w * np.exp2(127.0 - byte)[:, None, :]).reshape(k, n).astype(np.float32)
    by_word = np.ascontiguousarray(scaled.reshape(k // 512, 128, 4, n).transpose(0, 1, 3, 2))
    if fmt == "e4m3":
        words = by_word.astype(ml_dtypes.float8_e4m3fn).view(np.uint8)
    else:
        c = by_word.astype(ml_dtypes.float4_e2m1fn).view(np.uint8) & 0xF
        words = (c[..., 0::2] | (c[..., 1::2] << 4)).reshape(k // 512, 128, 2 * n)
    return np.ascontiguousarray(words), np.ascontiguousarray(byte.astype(np.uint8).reshape(k // 512, 16, n))


def unpack_weight(words, scales, fmt):
    g, _, n = scales.shape
    words = np.ascontiguousarray(words).reshape(g, 128, n, -1)
    if fmt == "e4m3":
        vals = words.view(ml_dtypes.float8_e4m3fn).astype(np.float64)
    else:
        nib = np.empty((g, 128, n, 4), np.uint8)
        nib[..., 0::2] = words & 0xF
        nib[..., 1::2] = words >> 4
        vals = E2M1[nib]
    vals = vals * np.repeat(np.exp2(scales.astype(np.float64) - 127.0), 8, axis=1)[..., None]
    return vals.transpose(0, 1, 3, 2).reshape(g * 512, n)


def gelu(v):
    return 0.5 * v * (1.0 + np.tanh(np.sqrt(2.0 / np.pi) * (v + 0.044715 * v**3)))


def pack_table4(v):
    words, scales = pack_weight(v, "e2m1")
    g, t = words.shape[0] // 2, v.shape[1]
    words = words.reshape(g, 2, 128, t, 2).transpose(0, 2, 3, 1, 4)
    return np.concatenate([words.reshape(g, -1), scales.reshape(g, -1)], axis=1)


def unpack_table4(tab):
    g, t = tab.shape[0], tab.shape[1] // 544
    words = tab[:, :512 * t].reshape(g, 128, t, 2, 2).transpose(0, 3, 1, 2, 4).reshape(2 * g, 128, 2 * t)
    return unpack_weight(words, tab[:, 512 * t:].reshape(2 * g, 16, t), "e2m1")


K, T, S, H, N = 1024, 2048, 1024, 1024, 512

def setup_inputs():
    n = np.random.standard_normal
    s = mx_kscale(K)[:, None]
    u = mx_kscale(H)[:, None]
    tab = pack_table4(n((K, T)) * s)
    a = (n((K, H)) / np.sqrt(K) / s * u.T).astype(np.float32)
    d = (0.5 * n(H) * u[:, 0]).astype(np.float32)
    c4_words, c4_scales = pack_weight(n((H, N)) / np.sqrt(H) / u, "e2m1")
    r = (0.5 * n(N)).astype(np.float32)
    q = np.random.uniform(0.5, 2.0, N).astype(np.float32)
    offs = striped(np.random.permutation(T)[:S])
    return {"tab": tab, "offs": offs, "a": a, "d": d,
            "c4_words": c4_words, "c4_scales": c4_scales, "r": r, "q": q}

def reference(tab, offs, a, d, c4_words, c4_scales, r, q):
    v = unpack_table4(tab)[:, unstriped(offs)]
    aq = mxq(f64(a), 0, "e4m3")
    h = (aq.T @ v) + f64(d)[:, None]
    hq = mxq(h, 0, "e4m3")
    c4 = unpack_weight(c4_words, c4_scales, "e2m1")
    y = c4.T @ hq
    e = y - f64(r)[:, None]
    return f64(q)[:, None] * np.square(e)

@@ -1,0 +1,179 @@
+from contextlib import ExitStack
+
+import concourse.mybir as mybir
+
+K, T, S, H, N = 1024, 2048, 1024, 1024, 512
+FLOPS = 2 * K * H * S + 2 * H * N * S
+
+F32 = mybir.dt.float32
+BF16 = mybir.dt.bfloat16
+I32 = mybir.dt.int32
+U32 = mybir.dt.uint32
+U16 = mybir.dt.uint16
+U8 = mybir.dt.uint8
+FP8X4 = mybir.dt.float8_e4m3fn_x4
+FP4X4 = mybir.dt.float4_e2m1fn_x4
+ALU = mybir.AluOpType
+ACT = mybir.ActivationFunctionType
+
+P = 128
+PACK = 4
+PASS = P * PACK
+HALF = 512
+CHUNK = 128
+PAIR = 256
+LIVE = 24
+RAW_BYTES = PACK * PASS * 4
+VECTOR_FROM = {(0, 0): 96, (0, 1): 44, (1, 0): 128, (1, 1): 128}
+
+
+def tile_list_logged_state_cost_kernel(tc, tab, offs, a, d, c4_words, c4_scales, r, q, out):
+    nc = tc.nc
+    with ExitStack() as ctx:
+        keep = ctx.enter_context(tc.tile_pool(name="keep", bufs=1))
+        shared = ctx.enter_context(tc.tile_pool(name="shared", bufs=1))
+        psum = ctx.enter_context(tc.psum_pool(name="psum", bufs=8))
+
+        offsets = keep.tile([P, S // 16], U16, name="offsets")
+        nc.sync.dma_start(offsets[:], offs)
+
+        drift = keep.tile([P, 2, PACK], F32, name="drift")
+        nc.sync.dma_start(drift[:], d.rearrange("(b p t) -> p b t", b=2, t=PACK))
+
+        scale_window = keep.tile([P, T], U8, name="scale_window", align_bytes=64)
+        tab_scales = tab[0, 512 * T : 544 * T].rearrange("(g q t) -> g q t", g=2, q=16)
+        for quad in range(4):
+            nc.scalar.dma_start(
+                scale_window[32 * quad + LIVE : 32 * quad + 32, :].bitcast(I32),
+                tab_scales[:, 4 * quad : 4 * quad + 4, :].bitcast(I32),
+            )
+            nc.vector.memset(scale_window[32 * quad : 32 * quad + LIVE, :].bitcast(I32), 0)
+
+        word_window = shared.tile([P, T], I32, name="word_window", align_bytes=64, offset=RAW_BYTES // 2)
+        nc.scalar.dma_start(word_window[:], tab[0, 0 : 512 * T].rearrange("(p x) -> p x", p=P).bitcast(I32))
+
+        def load_raw(queue, tile, b, g):
+            queue.dma_start(
+                tile[:],
+                a[g * PASS : (g + 1) * PASS, b * PASS : (b + 1) * PASS].rearrange("(p j) i -> p j i", j=PACK),
+            )
+
+        raw = {}
+        for g in range(2):
+            raw[0, g] = keep.tile([P, PACK, PASS], F32, name="raw0%d" % g)
+            load_raw(nc.scalar, raw[0, g], 0, g)
+
+        v_scales = []
+        for g in range(2):
+            plane = keep.tile([P, S // 4], I32, name="v_scales%d" % g, align_bytes=64)
+            nc.vector.memset(plane[:], 0)
+            v_scales.append(plane)
+        picked_scales = keep.tile([P, S], U8, name="picked_scales", align_bytes=64)
+        nc.vector.tensor_copy(picked_scales[:], scale_window[:].indirect(offsets[:]))
+        for g in range(2):
+            first = LIVE + 4 * g
+            nc.sync.dma_start(v_scales[g][0 : P - first, :], picked_scales[first:P, :].bitcast(I32))
+
+        picked = keep.tile([P, S], U32, name="picked", align_bytes=64)
+        nc.vector.tensor_copy(picked[:], word_window[:].bitcast(U32).indirect(offsets[:]))
+        for g in range(2):
+            raw[1, g] = shared.tile([P, PACK, PASS], F32, name="raw1%d" % g, align_bytes=64, offset=g * RAW_BYTES)
+            load_raw(nc.sync, raw[1, g], 1, g)
+        v_words = []
+        for half in range(2):
+            parted = keep.tile([P, 2, HALF], U16, name="parted%d" % half, align_bytes=64)
+            pairs = picked[:, half * HALF : (half + 1) * HALF].bitcast(U16)
+            nc.vector.tensor_copy(parted[:], pairs.rearrange("p (n g) -> p g n", g=2))
+            v_words.append(parted)
+
+        a_codes, a_scales = {}, {}
+        for b in range(2):
+            for g in range(2):
+                grouped = keep.tile([P, PACK * PASS], BF16, name="grouped%d%d" % (b, g), align_bytes=64)
+                src = raw[b, g][:].rearrange("p j (m t) -> p m j t", t=PACK)
+                dst = grouped[:].rearrange("p (t m j) -> p m j t", t=PACK, j=PACK)
+                cut = VECTOR_FROM[b, g]
+                nc.scalar.copy(dst[:, 0:cut], src[:, 0:cut])
+                if cut < P:
+                    nc.vector.tensor_copy(dst[:, cut:P], src[:, cut:P])
+                a_codes[b, g] = keep.tile([P, PASS], U32, name="a_codes%d%d" % (b, g), align_bytes=64)
+                a_scales[b, g] = keep.tile([P, PASS], U8, name="a_scales%d%d" % (b, g), align_bytes=64)
+                nc.vector.quantize_mx(out=a_codes[b, g][:].bitcast(FP8X4), scales=a_scales[b, g][:], in_=grouped[:])
+
+        c_words = shared.tile([P, 2, N // 2], I32, name="c_words", align_bytes=64, offset=0)
+        nc.sync.dma_start(c_words[:], c4_words.rearrange("b p x -> p b x").bitcast(I32))
+        weight = shared.tile([P, 4], F32, name="weight", align_bytes=64, offset=3072)
+        setpoint = shared.tile([P, 4], F32, name="setpoint", align_bytes=64, offset=3136)
+        with nc.allow_non_contiguous_dma(reason="one value a partition"):
+            nc.sync.dma_start(weight[:], q.rearrange("(c p) -> p c", p=P))
+            nc.sync.dma_start(setpoint[:], r.rearrange("(c p) -> p c", p=P))
+        c_scales = shared.tile([P, 2, N // 4], I32, name="c_scales", align_bytes=64, offset=2048)
+        nc.gpsimd.memset(c_scales[:], 0)
+        for quad in range(4):
+            nc.sync.dma_start(
+                c_scales[32 * quad : 32 * quad + 4, :, :],
+                c4_scales[:, 4 * quad : 4 * quad + 4, :].rearrange("b r c -> r b c").bitcast(I32),
+            )
+        halves = keep.tile([P, 4], F32, name="halves")
+        root = keep.tile([P, 4], F32, name="root")
+        scaled = keep.tile([P, 4], F32, name="scaled")
+        shift = keep.tile([P, 4], F32, name="shift")
+        nc.gpsimd.memset(halves[:], 0.5)
+        nc.gpsimd.tensor_tensor(root[:], weight[:], halves[:], ALU.pow)
+        nc.gpsimd.tensor_tensor(scaled[:], setpoint[:], root[:], ALU.mult)
+        nc.gpsimd.tensor_scalar(shift[:], scaled[:], -1.0, 0.0, ALU.mult, ALU.add)
+
+        h_codes, h_scales = {}, {}
+        for b in range(2):
+            banks = [psum.tile([P, PACK, CHUNK], F32, name="bank", tag="bank") for c in range(S // CHUNK)]
+            for g in range(2):
+                for c in range(S // CHUNK):
+                    half, col = divmod(c * CHUNK, HALF)
+                    for t in range(PACK):
+                        nc.tensor.matmul_mx(
+                            out=banks[c][:, t, :],
+                            lhsT=a_codes[b, g][:, t * P : (t + 1) * P].bitcast(FP8X4),
+                            lhsT_scale=a_scales[b, g][:, t * P : (t + 1) * P],
+                            rhs=v_words[half][:, g, col : col + CHUNK].bitcast(FP4X4),
+                            rhs_scale=v_scales[g][:].bitcast(U8)[:, c * CHUNK : (c + 1) * CHUNK],
+                            start=(g == 0 and t == 0),
+                            stop=(g == 1 and t == PACK - 1),
+                        )
+            for half in range(2):
+                h_codes[b, half] = keep.tile([P, HALF], U32, name="h_codes%d%d" % (b, half), align_bytes=64)
+                h_scales[b, half] = keep.tile([P, HALF], U8, name="h_scales%d%d" % (b, half), align_bytes=64)
+            for pair in range(S // PAIR):
+                rounded = keep.tile([P, PAIR, PACK], BF16, name="rounded%d%d" % (b, pair), align_bytes=64)
+                for u in range(2):
+                    nc.vector.tensor_tensor(
+                        rounded[:, u * CHUNK : (u + 1) * CHUNK, :],
+                        banks[2 * pair + u][:].rearrange("p t n -> p n t"),
+                        drift[:, b : b + 1, :].to_broadcast([P, CHUNK, PACK]),
+                        ALU.add,
+                    )
+                half, col = divmod(pair * PAIR, HALF)
+                nc.vector.quantize_mx(
+                    out=h_codes[b, half][:, col : col + PAIR].bitcast(FP8X4),
+                    scales=h_scales[b, half][:, col : col + PAIR],
+                    in_=rounded[:].rearrange("p n t -> p (n t)"),
+                )
+
+        for half in range(2):
+            banks = [psum.tile([P, HALF], F32, name="bank", tag="bank") for c in range(N // P)]
+            for b in range(2):
+                for c in range(N // P):
+                    nc.tensor.matmul_mx(
+                        out=banks[c][:],
+                        lhsT=c_words[:, b, c * P // 2 : (c + 1) * P // 2].bitcast(FP4X4),
+                        lhsT_scale=c_scales[:, b, c * P // 4 : (c + 1) * P // 4].bitcast(U8),
+                        rhs=h_codes[b, half][:].bitcast(FP8X4),
+                        rhs_scale=h_scales[b, half][:],
+                        start=(b == 0),
+                        stop=(b == 1),
+                    )
+            for c in range(N // P):
+                cost = keep.tile([P, HALF], F32, name="cost%d%d" % (half, c))
+                nc.scalar.activation(
+                    cost[:], banks[c][:], ACT.Square, bias=shift[:, c : c + 1], scale=root[:, c : c + 1]
+                )
+                nc.sync.dma_start(out[c * P : (c + 1) * P, half * HALF : (half + 1) * HALF], cost[:])

@@ -22,9 +22,11 @@ PASS = P * PACK
 HALF = 512
 CHUNK = 128
 PAIR = 256
-LIVE = 24
+QUARTER = 256
+LIVE = 96
 RAW_BYTES = PACK * PASS * 4
-VECTOR_FROM = {(0, 0): 96, (0, 1): 44, (1, 0): 128, (1, 1): 128}
+REUSES = {(0, 0, 1): "grouped101", (0, 1, 0): "grouped111"}
+ON_VECTOR = ((0, 0, 0), (0, 1, 1))
 
 
 def tile_list_logged_state_cost_kernel(tc, tab, offs, a, d, c4_words, c4_scales, r, q, out):
@@ -37,31 +39,27 @@ def tile_list_logged_state_cost_kernel(tc, tab, offs, a, d, c4_words, c4_scales,
         offsets = keep.tile([P, S // 16], U16, name="offsets")
         nc.sync.dma_start(offsets[:], offs)
 
-        drift = keep.tile([P, 2, PACK], F32, name="drift")
-        nc.sync.dma_start(drift[:], d.rearrange("(b p t) -> p b t", b=2, t=PACK))
+        scale_window = shared.tile([P, T], U8, name="scale_window", align_bytes=64, offset=RAW_BYTES - T // 2)
+        nc.sync.dma_start(
+            scale_window[LIVE:P, :].bitcast(I32),
+            tab[0, 512 * T : 544 * T].rearrange("(x t) -> x t", t=T).bitcast(I32),
+        )
+        nc.vector.memset(scale_window[0:64, :].bitcast(I32), 0)
+        nc.vector.memset(scale_window[64:LIVE, :].bitcast(I32), 0)
 
-        scale_window = keep.tile([P, T], U8, name="scale_window", align_bytes=64)
-        tab_scales = tab[0, 512 * T : 544 * T].rearrange("(g q t) -> g q t", g=2, q=16)
-        for quad in range(4):
-            nc.scalar.dma_start(
-                scale_window[32 * quad + LIVE : 32 * quad + 32, :].bitcast(I32),
-                tab_scales[:, 4 * quad : 4 * quad + 4, :].bitcast(I32),
-            )
-            nc.vector.memset(scale_window[32 * quad : 32 * quad + LIVE, :].bitcast(I32), 0)
-
-        word_window = shared.tile([P, T], I32, name="word_window", align_bytes=64, offset=RAW_BYTES // 2)
-        nc.scalar.dma_start(word_window[:], tab[0, 0 : 512 * T].rearrange("(p x) -> p x", p=P).bitcast(I32))
-
-        def load_raw(queue, tile, b, g):
-            queue.dma_start(
+        def load_raw(tile, b, g):
+            nc.sync.dma_start(
                 tile[:],
                 a[g * PASS : (g + 1) * PASS, b * PASS : (b + 1) * PASS].rearrange("(p j) i -> p j i", j=PACK),
             )
 
         raw = {}
-        for g in range(2):
-            raw[0, g] = keep.tile([P, PACK, PASS], F32, name="raw0%d" % g)
-            load_raw(nc.scalar, raw[0, g], 0, g)
+        raw[0, 0] = shared.tile([P, PACK, PASS], F32, name="raw00", align_bytes=64, offset=2 * RAW_BYTES)
+        load_raw(raw[0, 0], 0, 0)
+        word_window = keep.tile([P, T], I32, name="word_window", align_bytes=64)
+        nc.sync.dma_start(word_window[:], tab[0, 0 : 512 * T].rearrange("(p x) -> p x", p=P).bitcast(I32))
+        drift = keep.tile([P, 2, PACK], F32, name="drift")
+        nc.sync.dma_start(drift[:], d.rearrange("(b p t) -> p b t", b=2, t=PACK))
 
         v_scales = []
         for g in range(2):
@@ -71,34 +69,51 @@ def tile_list_logged_state_cost_kernel(tc, tab, offs, a, d, c4_words, c4_scales,
         picked_scales = keep.tile([P, S], U8, name="picked_scales", align_bytes=64)
         nc.vector.tensor_copy(picked_scales[:], scale_window[:].indirect(offsets[:]))
         for g in range(2):
-            first = LIVE + 4 * g
-            nc.sync.dma_start(v_scales[g][0 : P - first, :], picked_scales[first:P, :].bitcast(I32))
-
-        picked = keep.tile([P, S], U32, name="picked", align_bytes=64)
-        nc.vector.tensor_copy(picked[:], word_window[:].bitcast(U32).indirect(offsets[:]))
-        for g in range(2):
-            raw[1, g] = shared.tile([P, PACK, PASS], F32, name="raw1%d" % g, align_bytes=64, offset=g * RAW_BYTES)
-            load_raw(nc.sync, raw[1, g], 1, g)
-        v_words = []
-        for half in range(2):
-            parted = keep.tile([P, 2, HALF], U16, name="parted%d" % half, align_bytes=64)
-            pairs = picked[:, half * HALF : (half + 1) * HALF].bitcast(U16)
-            nc.vector.tensor_copy(parted[:], pairs.rearrange("p (n g) -> p g n", g=2))
-            v_words.append(parted)
+            for quad in range(4):
+                first = LIVE + 16 * g + 4 * quad
+                nc.sync.dma_start(
+                    v_scales[g][32 * quad : 32 * quad + 4, :], picked_scales[first : first + 4, :].bitcast(I32)
+                )
+            b, k = (0, 1) if g == 0 else (1, 0)
+            raw[b, k] = shared.tile(
+                [P, PACK, PASS], F32, name="raw%d%d" % (b, k), align_bytes=64, offset=g * RAW_BYTES
+            )
+            load_raw(raw[b, k], b, k)
 
         a_codes, a_scales = {}, {}
-        for b in range(2):
-            for g in range(2):
-                grouped = keep.tile([P, PACK * PASS], BF16, name="grouped%d%d" % (b, g), align_bytes=64)
-                src = raw[b, g][:].rearrange("p j (m t) -> p m j t", t=PACK)
-                dst = grouped[:].rearrange("p (t m j) -> p m j t", t=PACK, j=PACK)
-                cut = VECTOR_FROM[b, g]
-                nc.scalar.copy(dst[:, 0:cut], src[:, 0:cut])
-                if cut < P:
-                    nc.vector.tensor_copy(dst[:, cut:P], src[:, cut:P])
-                a_codes[b, g] = keep.tile([P, PASS], U32, name="a_codes%d%d" % (b, g), align_bytes=64)
-                a_scales[b, g] = keep.tile([P, PASS], U8, name="a_scales%d%d" % (b, g), align_bytes=64)
-                nc.vector.quantize_mx(out=a_codes[b, g][:].bitcast(FP8X4), scales=a_scales[b, g][:], in_=grouped[:])
+
+        def quantize_a(b, g):
+            src = raw[b, g][:].rearrange("p j (m u t) -> p u m j t", u=2, t=2)
+            for u in range(2):
+                name = "%d%d%d" % (b, g, u)
+                grouped = keep.tile([P, 2 * PASS], BF16, name="grouped" + name, tag="grouped" + name, align_bytes=64)
+                dst = grouped[:].rearrange("p (t m j) -> p m j t", t=2, j=PACK)
+                if (b, g, u) in ON_VECTOR:
+                    nc.vector.tensor_copy(dst, src[:, u])
+                else:
+                    nc.scalar.copy(dst, src[:, u])
+                codes = keep.tile([P, 2 * P], U32, name="a_codes" + name, align_bytes=64)
+                scales = keep.tile([P, 2 * P], U8, name="a_scales" + name, align_bytes=64)
+                nc.vector.quantize_mx(out=codes[:].bitcast(FP8X4), scales=scales[:], in_=grouped[:])
+                for t in range(2):
+                    a_codes[b, g, 2 * u + t] = codes[:, t * P : (t + 1) * P]
+                    a_scales[b, g, 2 * u + t] = scales[:, t * P : (t + 1) * P]
+
+        quantize_a(0, 0)
+        raw[1, 1] = shared.tile([P, PACK, PASS], F32, name="raw11", align_bytes=64, offset=2 * RAW_BYTES)
+        load_raw(raw[1, 1], 1, 1)
+
+        v_words = [keep.tile([P, 2, HALF], U16, name="parted%d" % half, align_bytes=64) for half in range(2)]
+        for part in range(S // QUARTER):
+            picked = keep.tile([P, QUARTER], U32, name="picked%d" % part, align_bytes=64)
+            nc.vector.tensor_copy(
+                picked[:], word_window[:].bitcast(U32).indirect(offsets[:, 16 * part : 16 * part + 16])
+            )
+            half, col = divmod(part * QUARTER, HALF)
+            nc.vector.tensor_copy(
+                v_words[half][:, :, col : col + QUARTER], picked[:].bitcast(U16).rearrange("p (n g) -> p g n", g=2)
+            )
+        quantize_a(0, 1)
 
         c_words = shared.tile([P, 2, N // 2], I32, name="c_words", align_bytes=64, offset=0)
         nc.sync.dma_start(c_words[:], c4_words.rearrange("b p x -> p b x").bitcast(I32))
@@ -123,40 +138,72 @@ def tile_list_logged_state_cost_kernel(tc, tab, offs, a, d, c4_words, c4_scales,
         nc.gpsimd.tensor_tensor(scaled[:], setpoint[:], root[:], ALU.mult)
         nc.gpsimd.tensor_scalar(shift[:], scaled[:], -1.0, 0.0, ALU.mult, ALU.add)
 
+        quantize_a(1, 0)
+        quantize_a(1, 1)
+
+        def first_pass(bank, b, g, t, first, width, start, stop):
+            half, col = divmod(first, HALF)
+            nc.tensor.matmul_mx(
+                out=bank,
+                lhsT=a_codes[b, g, t].bitcast(FP8X4),
+                lhsT_scale=a_scales[b, g, t],
+                rhs=v_words[half][:, g, col : col + width].bitcast(FP4X4),
+                rhs_scale=v_scales[g][:].bitcast(U8)[:, first : first + width],
+                start=start,
+                stop=stop,
+            )
+
         h_codes, h_scales = {}, {}
         for b in range(2):
-            banks = [psum.tile([P, PACK, CHUNK], F32, name="bank", tag="bank") for c in range(S // CHUNK)]
+            wide = (0,) if b == 1 else ()
+            banks = [psum.tile([P, PACK, CHUNK], F32, name="bank", tag="bank") for c in range(8)]
             for g in range(2):
-                for c in range(S // CHUNK):
-                    half, col = divmod(c * CHUNK, HALF)
-                    for t in range(PACK):
-                        nc.tensor.matmul_mx(
-                            out=banks[c][:, t, :],
-                            lhsT=a_codes[b, g][:, t * P : (t + 1) * P].bitcast(FP8X4),
-                            lhsT_scale=a_scales[b, g][:, t * P : (t + 1) * P],
-                            rhs=v_words[half][:, g, col : col + CHUNK].bitcast(FP4X4),
-                            rhs_scale=v_scales[g][:].bitcast(U8)[:, c * CHUNK : (c + 1) * CHUNK],
-                            start=(g == 0 and t == 0),
-                            stop=(g == 1 and t == PACK - 1),
-                        )
+                for half in range(2):
+                    for u in range(4):
+                        bank = banks[4 * half + u]
+                        if half in wide:
+                            first_pass(bank[:].rearrange("p t n -> p (t n)"), b, g, u, half * HALF, HALF, g == 0, g == 1)
+                        else:
+                            for t in range(PACK):
+                                first_pass(
+                                    bank[:, t, :], b, g, t, half * HALF + u * CHUNK, CHUNK,
+                                    g == 0 and t == 0, g == 1 and t == PACK - 1,
+                                )
             for half in range(2):
                 h_codes[b, half] = keep.tile([P, HALF], U32, name="h_codes%d%d" % (b, half), align_bytes=64)
                 h_scales[b, half] = keep.tile([P, HALF], U8, name="h_scales%d%d" % (b, half), align_bytes=64)
-            for pair in range(S // PAIR):
-                rounded = keep.tile([P, PAIR, PACK], BF16, name="rounded%d%d" % (b, pair), align_bytes=64)
-                for u in range(2):
-                    nc.vector.tensor_tensor(
-                        rounded[:, u * CHUNK : (u + 1) * CHUNK, :],
-                        banks[2 * pair + u][:].rearrange("p t n -> p n t"),
-                        drift[:, b : b + 1, :].to_broadcast([P, CHUNK, PACK]),
-                        ALU.add,
+                if half in wide:
+                    planes = keep.tile([P, PACK, HALF], BF16, name="planes%d%d" % (b, half), align_bytes=64)
+                    for t in range(PACK):
+                        nc.scalar.activation(
+                            planes[:, t, :],
+                            banks[4 * half + t][:].rearrange("p t n -> p (t n)"),
+                            ACT.Identity,
+                            bias=drift[:, b, t : t + 1],
+                        )
+                for pair in range(2):
+                    col = pair * PAIR
+                    name = "rounded%d%d%d" % (b, half, pair)
+                    tag = REUSES.get((b, half, pair), name)
+                    rounded = keep.tile([P, PAIR, PACK], BF16, name=name, tag=tag, align_bytes=64)
+                    if half in wide:
+                        nc.vector.tensor_copy(
+                            rounded[:].rearrange("p (c i) t -> p c t i", i=4),
+                            planes[:, :, col : col + PAIR].rearrange("p t (c i) -> p c t i", i=4),
+                        )
+                    else:
+                        for u in range(2):
+                            nc.vector.tensor_tensor(
+                                rounded[:, u * CHUNK : (u + 1) * CHUNK, :],
+                                banks[4 * half + 2 * pair + u][:].rearrange("p t n -> p n t"),
+                                drift[:, b : b + 1, :].to_broadcast([P, CHUNK, PACK]),
+                                ALU.add,
+                            )
+                    nc.vector.quantize_mx(
+                        out=h_codes[b, half][:, col : col + PAIR].bitcast(FP8X4),
+                        scales=h_scales[b, half][:, col : col + PAIR],
+                        in_=rounded[:].rearrange("p n t -> p (n t)"),
                     )
-                half, col = divmod(pair * PAIR, HALF)
-                nc.vector.quantize_mx(
-                    out=h_codes[b, half][:, col : col + PAIR].bitcast(FP8X4),
-                    scales=h_scales[b, half][:, col : col + PAIR],
-                    in_=rounded[:].rearrange("p n t -> p (n t)"),
-                )
 
         for half in range(2):
             banks = [psum.tile([P, HALF], F32, name="bank", tag="bank") for c in range(N // P)]
@@ -173,7 +220,14 @@ def tile_list_logged_state_cost_kernel(tc, tab, offs, a, d, c4_words, c4_scales,
                     )
             for c in range(N // P):
                 cost = keep.tile([P, HALF], F32, name="cost%d%d" % (half, c))
-                nc.scalar.activation(
-                    cost[:], banks[c][:], ACT.Square, bias=shift[:, c : c + 1], scale=root[:, c : c + 1]
-                )
+                if (half, c) in ((1, 1),):
+                    deviation = keep.tile([P, HALF], F32, name="deviation%d%d" % (half, c))
+                    nc.vector.tensor_scalar(
+                        deviation[:], banks[c][:], root[:, c : c + 1], shift[:, c : c + 1], ALU.mult, ALU.add
+                    )
+                    nc.vector.tensor_tensor(cost[:], deviation[:], deviation[:], ALU.mult)
+                else:
+                    nc.scalar.activation(
+                        cost[:], banks[c][:], ACT.Square, bias=shift[:, c : c + 1], scale=root[:, c : c + 1]
+                    )
                 nc.sync.dma_start(out[c * P : (c + 1) * P, half * HALF : (half + 1) * HALF], cost[:])

@@ -19,14 +19,14 @@ ACT = mybir.ActivationFunctionType
 P = 128
 PACK = 4
 PASS = P * PACK
-HALF = 512
-CHUNK = 128
-PAIR = 256
-QUARTER = 256
-LIVE = 96
+HALF = S // 2
+CHUNK = HALF // PACK
+PIECE = 2 * CHUNK
+SCALE_ROWS = 96
 RAW_BYTES = PACK * PASS * 4
-REUSES = {(0, 0, 1): "grouped101", (0, 1, 0): "grouped111"}
-ON_VECTOR = ((0, 0, 0), (0, 1, 1))
+
+ROUNDED_ON_VECTOR = ((0, 1, 1), (1, 1, 0), (1, 1, 1))
+INTERLEAVED_ON_SCALAR = 0
 
 
 def tile_list_logged_state_cost_kernel(tc, tab, offs, a, d, c4_words, c4_scales, r, q, out):
@@ -41,44 +41,58 @@ def tile_list_logged_state_cost_kernel(tc, tab, offs, a, d, c4_words, c4_scales,
 
         scale_window = shared.tile([P, T], U8, name="scale_window", align_bytes=64, offset=RAW_BYTES - T // 2)
         nc.sync.dma_start(
-            scale_window[LIVE:P, :].bitcast(I32),
+            scale_window[SCALE_ROWS:P, :].bitcast(I32),
             tab[0, 512 * T : 544 * T].rearrange("(x t) -> x t", t=T).bitcast(I32),
         )
         nc.vector.memset(scale_window[0:64, :].bitcast(I32), 0)
-        nc.vector.memset(scale_window[64:LIVE, :].bitcast(I32), 0)
+        nc.vector.memset(scale_window[64:SCALE_ROWS, :].bitcast(I32), 0)
 
-        def load_raw(tile, b, g):
-            nc.sync.dma_start(
-                tile[:],
-                a[g * PASS : (g + 1) * PASS, b * PASS : (b + 1) * PASS].rearrange("(p j) i -> p j i", j=PACK),
-            )
-
-        raw = {}
-        raw[0, 0] = shared.tile([P, PACK, PASS], F32, name="raw00", align_bytes=64, offset=2 * RAW_BYTES)
-        load_raw(raw[0, 0], 0, 0)
         word_window = keep.tile([P, T], I32, name="word_window", align_bytes=64)
         nc.sync.dma_start(word_window[:], tab[0, 0 : 512 * T].rearrange("(p x) -> p x", p=P).bitcast(I32))
+
+        raw = {}
+
+        def load_a(b, g, offset):
+            raw[b, g] = shared.tile([P, PACK, PASS], F32, name="raw%d%d" % (b, g), align_bytes=64, offset=offset)
+            nc.sync.dma_start(
+                raw[b, g][:],
+                a[g * PASS : (g + 1) * PASS, b * PASS : (b + 1) * PASS].rearrange("(p j) c -> p j c", j=PACK),
+            )
+
+        load_a(0, 0, 2 * RAW_BYTES)
         drift = keep.tile([P, 2, PACK], F32, name="drift")
         nc.sync.dma_start(drift[:], d.rearrange("(b p t) -> p b t", b=2, t=PACK))
 
         v_scales = []
         for g in range(2):
-            plane = keep.tile([P, S // 4], I32, name="v_scales%d" % g, align_bytes=64)
-            nc.vector.memset(plane[:], 0)
-            v_scales.append(plane)
+            rows = keep.tile([P, S // 4], I32, name="v_scales%d" % g, align_bytes=64)
+            nc.vector.memset(rows[:], 0)
+            v_scales.append(rows)
         picked_scales = keep.tile([P, S], U8, name="picked_scales", align_bytes=64)
         nc.vector.tensor_copy(picked_scales[:], scale_window[:].indirect(offsets[:]))
-        for g in range(2):
+
+        def place_scales(g):
             for quad in range(4):
-                first = LIVE + 16 * g + 4 * quad
+                row = SCALE_ROWS + 16 * g + 4 * quad
                 nc.sync.dma_start(
-                    v_scales[g][32 * quad : 32 * quad + 4, :], picked_scales[first : first + 4, :].bitcast(I32)
+                    v_scales[g][32 * quad : 32 * quad + 4, :], picked_scales[row : row + 4, :].bitcast(I32)
                 )
-            b, k = (0, 1) if g == 0 else (1, 0)
-            raw[b, k] = shared.tile(
-                [P, PACK, PASS], F32, name="raw%d%d" % (b, k), align_bytes=64, offset=g * RAW_BYTES
-            )
-            load_raw(raw[b, k], b, k)
+
+        place_scales(0)
+        load_a(0, 1, 0)
+        place_scales(1)
+        load_a(1, 0, RAW_BYTES)
+
+        v_words = []
+        for half in range(2):
+            picked = keep.tile([P, HALF], U32, name="picked%d" % half, align_bytes=64)
+            columns = slice(half * HALF // 16, (half + 1) * HALF // 16)
+            nc.vector.tensor_copy(picked[:], word_window[:].bitcast(U32).indirect(offsets[:, columns]))
+            parted = keep.tile([P, 2, HALF], U16, name="parted%d" % half, align_bytes=64)
+            both = picked[:].bitcast(U16).rearrange("p (n g) -> p g n", g=2)
+            for g in range(2):
+                nc.vector.tensor_copy(parted[:, g, :], both[:, g, :])
+            v_words.append(parted)
 
         a_codes, a_scales = {}, {}
 
@@ -88,7 +102,7 @@ def tile_list_logged_state_cost_kernel(tc, tab, offs, a, d, c4_words, c4_scales,
                 name = "%d%d%d" % (b, g, u)
                 grouped = keep.tile([P, 2 * PASS], BF16, name="grouped" + name, tag="grouped" + name, align_bytes=64)
                 dst = grouped[:].rearrange("p (t m j) -> p m j t", t=2, j=PACK)
-                if (b, g, u) in ON_VECTOR:
+                if (b, g, u) in ROUNDED_ON_VECTOR:
                     nc.vector.tensor_copy(dst, src[:, u])
                 else:
                     nc.scalar.copy(dst, src[:, u])
@@ -100,25 +114,13 @@ def tile_list_logged_state_cost_kernel(tc, tab, offs, a, d, c4_words, c4_scales,
                     a_scales[b, g, 2 * u + t] = scales[:, t * P : (t + 1) * P]
 
         quantize_a(0, 0)
-        raw[1, 1] = shared.tile([P, PACK, PASS], F32, name="raw11", align_bytes=64, offset=2 * RAW_BYTES)
-        load_raw(raw[1, 1], 1, 1)
-
-        v_words = [keep.tile([P, 2, HALF], U16, name="parted%d" % half, align_bytes=64) for half in range(2)]
-        for part in range(S // QUARTER):
-            picked = keep.tile([P, QUARTER], U32, name="picked%d" % part, align_bytes=64)
-            nc.vector.tensor_copy(
-                picked[:], word_window[:].bitcast(U32).indirect(offsets[:, 16 * part : 16 * part + 16])
-            )
-            half, col = divmod(part * QUARTER, HALF)
-            nc.vector.tensor_copy(
-                v_words[half][:, :, col : col + QUARTER], picked[:].bitcast(U16).rearrange("p (n g) -> p g n", g=2)
-            )
+        load_a(1, 1, 2 * RAW_BYTES)
         quantize_a(0, 1)
 
         c_words = shared.tile([P, 2, N // 2], I32, name="c_words", align_bytes=64, offset=0)
         nc.sync.dma_start(c_words[:], c4_words.rearrange("b p x -> p b x").bitcast(I32))
-        weight = shared.tile([P, 4], F32, name="weight", align_bytes=64, offset=3072)
-        setpoint = shared.tile([P, 4], F32, name="setpoint", align_bytes=64, offset=3136)
+        weight = shared.tile([P, N // P], F32, name="weight", align_bytes=64, offset=3072)
+        setpoint = shared.tile([P, N // P], F32, name="setpoint", align_bytes=64, offset=3136)
         with nc.allow_non_contiguous_dma(reason="one value a partition"):
             nc.sync.dma_start(weight[:], q.rearrange("(c p) -> p c", p=P))
             nc.sync.dma_start(setpoint[:], r.rearrange("(c p) -> p c", p=P))
@@ -127,24 +129,25 @@ def tile_list_logged_state_cost_kernel(tc, tab, offs, a, d, c4_words, c4_scales,
         for quad in range(4):
             nc.sync.dma_start(
                 c_scales[32 * quad : 32 * quad + 4, :, :],
-                c4_scales[:, 4 * quad : 4 * quad + 4, :].rearrange("b r c -> r b c").bitcast(I32),
+                c4_scales[:, 4 * quad : 4 * quad + 4, :].rearrange("b m c -> m b c").bitcast(I32),
             )
-        halves = keep.tile([P, 4], F32, name="halves")
-        root = keep.tile([P, 4], F32, name="root")
-        scaled = keep.tile([P, 4], F32, name="scaled")
-        shift = keep.tile([P, 4], F32, name="shift")
-        nc.gpsimd.memset(halves[:], 0.5)
-        nc.gpsimd.tensor_tensor(root[:], weight[:], halves[:], ALU.pow)
+
+        exponent = keep.tile([P, N // P], F32, name="exponent")
+        root = keep.tile([P, N // P], F32, name="root")
+        scaled = keep.tile([P, N // P], F32, name="scaled")
+        shift = keep.tile([P, N // P], F32, name="shift")
+        nc.gpsimd.memset(exponent[:], 0.5)
+        nc.gpsimd.tensor_tensor(root[:], weight[:], exponent[:], ALU.pow)
         nc.gpsimd.tensor_tensor(scaled[:], setpoint[:], root[:], ALU.mult)
         nc.gpsimd.tensor_scalar(shift[:], scaled[:], -1.0, 0.0, ALU.mult, ALU.add)
 
         quantize_a(1, 0)
         quantize_a(1, 1)
 
-        def first_pass(bank, b, g, t, first, width, start, stop):
+        def first_pass(sums, b, g, t, first, width, start, stop):
             half, col = divmod(first, HALF)
             nc.tensor.matmul_mx(
-                out=bank,
+                out=sums,
                 lhsT=a_codes[b, g, t].bitcast(FP8X4),
                 lhsT_scale=a_scales[b, g, t],
                 rhs=v_words[half][:, g, col : col + width].bitcast(FP4X4),
@@ -153,81 +156,105 @@ def tile_list_logged_state_cost_kernel(tc, tab, offs, a, d, c4_words, c4_scales,
                 stop=stop,
             )
 
-        h_codes, h_scales = {}, {}
-        for b in range(2):
-            wide = (0,) if b == 1 else ()
-            banks = [psum.tile([P, PACK, CHUNK], F32, name="bank", tag="bank") for c in range(8)]
-            for g in range(2):
-                for half in range(2):
-                    for u in range(4):
-                        bank = banks[4 * half + u]
-                        if half in wide:
-                            first_pass(bank[:].rearrange("p t n -> p (t n)"), b, g, u, half * HALF, HALF, g == 0, g == 1)
-                        else:
-                            for t in range(PACK):
-                                first_pass(
-                                    bank[:, t, :], b, g, t, half * HALF + u * CHUNK, CHUNK,
-                                    g == 0 and t == 0, g == 1 and t == PACK - 1,
-                                )
-            for half in range(2):
-                h_codes[b, half] = keep.tile([P, HALF], U32, name="h_codes%d%d" % (b, half), align_bytes=64)
-                h_scales[b, half] = keep.tile([P, HALF], U8, name="h_scales%d%d" % (b, half), align_bytes=64)
-                if half in wide:
-                    planes = keep.tile([P, PACK, HALF], BF16, name="planes%d%d" % (b, half), align_bytes=64)
+        def narrow_product(b):
+            banks = [psum.tile([P, PACK, CHUNK], F32, name="bank", tag="bank") for chunk in range(HALF // CHUNK)]
+            for chunk, bank in enumerate(banks):
+                for g in range(2):
                     for t in range(PACK):
-                        nc.scalar.activation(
-                            planes[:, t, :],
-                            banks[4 * half + t][:].rearrange("p t n -> p (t n)"),
-                            ACT.Identity,
-                            bias=drift[:, b, t : t + 1],
-                        )
-                for pair in range(2):
-                    col = pair * PAIR
-                    name = "rounded%d%d%d" % (b, half, pair)
-                    tag = REUSES.get((b, half, pair), name)
-                    rounded = keep.tile([P, PAIR, PACK], BF16, name=name, tag=tag, align_bytes=64)
-                    if half in wide:
-                        nc.vector.tensor_copy(
-                            rounded[:].rearrange("p (c i) t -> p c t i", i=4),
-                            planes[:, :, col : col + PAIR].rearrange("p t (c i) -> p c t i", i=4),
-                        )
-                    else:
-                        for u in range(2):
-                            nc.vector.tensor_tensor(
-                                rounded[:, u * CHUNK : (u + 1) * CHUNK, :],
-                                banks[4 * half + 2 * pair + u][:].rearrange("p t n -> p n t"),
-                                drift[:, b : b + 1, :].to_broadcast([P, CHUNK, PACK]),
-                                ALU.add,
-                            )
-                    nc.vector.quantize_mx(
-                        out=h_codes[b, half][:, col : col + PAIR].bitcast(FP8X4),
-                        scales=h_scales[b, half][:, col : col + PAIR],
-                        in_=rounded[:].rearrange("p n t -> p (n t)"),
-                    )
+                        start, stop = (g, t) == (0, 0), (g, t) == (1, PACK - 1)
+                        first_pass(bank[:, t, :], b, g, t, chunk * CHUNK, CHUNK, start, stop)
+            return banks
 
-        for half in range(2):
-            banks = [psum.tile([P, HALF], F32, name="bank", tag="bank") for c in range(N // P)]
-            for b in range(2):
-                for c in range(N // P):
-                    nc.tensor.matmul_mx(
-                        out=banks[c][:],
-                        lhsT=c_words[:, b, c * P // 2 : (c + 1) * P // 2].bitcast(FP4X4),
-                        lhsT_scale=c_scales[:, b, c * P // 4 : (c + 1) * P // 4].bitcast(U8),
-                        rhs=h_codes[b, half][:].bitcast(FP8X4),
-                        rhs_scale=h_scales[b, half][:],
-                        start=(b == 0),
-                        stop=(b == 1),
-                    )
+        def wide_product(b):
+            banks = [psum.tile([P, HALF], F32, name="bank", tag="bank") for t in range(PACK)]
+            for t, bank in enumerate(banks):
+                for g in range(2):
+                    first_pass(bank[:], b, g, t, HALF, HALF, g == 0, g == 1)
+            return banks
+
+        h_codes, h_scales = {}, {}
+
+        def quantize_h(b, piece, rounded):
+            h_codes[b, piece] = keep.tile([P, PIECE], U32, name="h_codes%d%d" % (b, piece), align_bytes=64)
+            h_scales[b, piece] = keep.tile([P, PIECE], U8, name="h_scales%d%d" % (b, piece), align_bytes=64)
+            nc.vector.quantize_mx(
+                out=h_codes[b, piece][:].bitcast(FP8X4),
+                scales=h_scales[b, piece][:],
+                in_=rounded[:].rearrange("p n t -> p (n t)"),
+            )
+
+        def narrow_finish(b, piece, banks, tag):
+            rounded = keep.tile([P, PIECE, PACK], BF16, name="rounded", tag=tag, align_bytes=64)
+            for u in range(2):
+                nc.vector.tensor_tensor(
+                    rounded[:, u * CHUNK : (u + 1) * CHUNK, :],
+                    banks[2 * piece + u][:].rearrange("p t n -> p n t"),
+                    drift[:, b : b + 1, :].to_broadcast([P, CHUNK, PACK]),
+                    ALU.add,
+                )
+            quantize_h(b, piece, rounded)
+
+        def wide_drain(b, banks, offset):
+            tiles = shared.tile([P, PACK, HALF], BF16, name="tiles%d" % b, align_bytes=64, offset=offset)
+            for t in range(PACK):
+                nc.scalar.activation(tiles[:, t, :], banks[t][:], ACT.Identity, bias=drift[:, b, t : t + 1])
+            return tiles
+
+        def wide_finish(b, piece, tiles):
+            rounded = keep.tile([P, PIECE, PACK], BF16, name="rounded%d%d" % (b, piece), align_bytes=64)
+            col = piece * PIECE - HALF
+            dst = rounded[:].rearrange("p (c i) t -> p c t i", i=4)
+            src = tiles[:, :, col : col + PIECE].rearrange("p t (c i) -> p c t i", i=4)
+            if b == INTERLEAVED_ON_SCALAR:
+                nc.scalar.copy(dst, src)
+            else:
+                nc.vector.tensor_copy(dst, src)
+            quantize_h(b, piece, rounded)
+
+        def second_product(piece, on_vector):
+            banks = [psum.tile([P, 2, PIECE], F32, name="bank", tag="bank") for pair in range(2)]
+            for pair, bank in enumerate(banks):
+                for b in range(2):
+                    for u in range(2):
+                        c = 2 * pair + u
+                        for col in range(0, PIECE, CHUNK):
+                            nc.tensor.matmul_mx(
+                                out=bank[:, u, col : col + CHUNK],
+                                lhsT=c_words[:, b, c * P // 2 : (c + 1) * P // 2].bitcast(FP4X4),
+                                lhsT_scale=c_scales[:, b, c * P // 4 : (c + 1) * P // 4].bitcast(U8),
+                                rhs=h_codes[b, piece][:, col : col + CHUNK].bitcast(FP8X4),
+                                rhs_scale=h_scales[b, piece][:, col : col + CHUNK],
+                                start=(b, u, col) == (0, 0, 0),
+                                stop=(b, u, col) == (1, 1, PIECE - CHUNK),
+                            )
             for c in range(N // P):
-                cost = keep.tile([P, HALF], F32, name="cost%d%d" % (half, c))
-                if (half, c) in ((1, 1),):
-                    deviation = keep.tile([P, HALF], F32, name="deviation%d%d" % (half, c))
+                sums = banks[c // 2][:, c % 2, :]
+                cost = keep.tile([P, PIECE], F32, name="cost%d%d" % (piece, c))
+                if c in on_vector:
+                    deviation = keep.tile([P, PIECE], F32, name="deviation%d" % c)
                     nc.vector.tensor_scalar(
-                        deviation[:], banks[c][:], root[:, c : c + 1], shift[:, c : c + 1], ALU.mult, ALU.add
+                        deviation[:], sums, root[:, c : c + 1], shift[:, c : c + 1], ALU.mult, ALU.add
                     )
                     nc.vector.tensor_tensor(cost[:], deviation[:], deviation[:], ALU.mult)
                 else:
-                    nc.scalar.activation(
-                        cost[:], banks[c][:], ACT.Square, bias=shift[:, c : c + 1], scale=root[:, c : c + 1]
-                    )
-                nc.sync.dma_start(out[c * P : (c + 1) * P, half * HALF : (half + 1) * HALF], cost[:])
+                    nc.scalar.activation(cost[:], sums, ACT.Square, bias=shift[:, c : c + 1], scale=root[:, c : c + 1])
+                nc.sync.dma_start(out[c * P : (c + 1) * P, piece * PIECE : (piece + 1) * PIECE], cost[:])
+
+        narrow0 = narrow_product(0)
+        wide0 = wide_product(0)
+        narrow_finish(0, 0, narrow0, "rounded00")
+        narrow1 = narrow_product(1)
+        tiles0 = wide_drain(0, wide0, 3 * RAW_BYTES // 2)
+        narrow_finish(1, 0, narrow1, "rounded10")
+        narrow_finish(0, 1, narrow0, "grouped111")
+        wide1 = wide_product(1)
+        wide_finish(0, 2, tiles0)
+        wide_finish(0, 3, tiles0)
+        tiles1 = wide_drain(1, wide1, 2 * RAW_BYTES)
+        second_product(0, ())
+        narrow_finish(1, 1, narrow1, "rounded11")
+        second_product(1, ())
+        wide_finish(1, 2, tiles1)
+        second_product(2, ())
+        wide_finish(1, 3, tiles1)
+        second_product(3, (0, 1))

@@ -22,11 +22,9 @@ PASS = P * PACK
 HALF = S // 2
 CHUNK = HALF // PACK
 PIECE = 2 * CHUNK
+SIDE = PASS // 2
 SCALE_ROWS = 96
-RAW_BYTES = PACK * PASS * 4
-
-ROUNDED_ON_VECTOR = ((0, 1, 1), (1, 1, 0), (1, 1, 1))
-INTERLEAVED_ON_SCALAR = 0
+RAW = PACK * SIDE * 4
 
 
 def tile_list_logged_state_cost_kernel(tc, tab, offs, a, d, c4_words, c4_scales, r, q, out):
@@ -34,12 +32,20 @@ def tile_list_logged_state_cost_kernel(tc, tab, offs, a, d, c4_words, c4_scales,
     with ExitStack() as ctx:
         keep = ctx.enter_context(tc.tile_pool(name="keep", bufs=1))
         shared = ctx.enter_context(tc.tile_pool(name="shared", bufs=1))
-        psum = ctx.enter_context(tc.psum_pool(name="psum", bufs=8))
+        psum = ctx.enter_context(tc.psum_pool(name="psum", bufs=1))
+
+        def sbuf(shape, dtype, name, on=None):
+            return keep.tile(shape, dtype, name=name, tag=on or name, align_bytes=64)
+
+        def placed(shape, dtype, name, offset):
+            return shared.tile(shape, dtype, name=name, align_bytes=64, offset=offset)
+
+        def bank(shape, number):
+            return psum.tile(shape, F32, name="bank%d" % number, tag="bank%d" % number)
 
         offsets = keep.tile([P, S // 16], U16, name="offsets")
         nc.sync.dma_start(offsets[:], offs)
-
-        scale_window = shared.tile([P, T], U8, name="scale_window", align_bytes=64, offset=RAW_BYTES - T // 2)
+        scale_window = placed([P, T], U8, "scale_window", RAW - T // 4)
         nc.sync.dma_start(
             scale_window[SCALE_ROWS:P, :].bitcast(I32),
             tab[0, 512 * T : 544 * T].rearrange("(x t) -> x t", t=T).bitcast(I32),
@@ -47,90 +53,129 @@ def tile_list_logged_state_cost_kernel(tc, tab, offs, a, d, c4_words, c4_scales,
         nc.vector.memset(scale_window[0:64, :].bitcast(I32), 0)
         nc.vector.memset(scale_window[64:SCALE_ROWS, :].bitcast(I32), 0)
 
-        word_window = keep.tile([P, T], I32, name="word_window", align_bytes=64)
+        word_window = placed([P, T], I32, "word_window", 3 * RAW)
         nc.sync.dma_start(word_window[:], tab[0, 0 : 512 * T].rearrange("(p x) -> p x", p=P).bitcast(I32))
 
         raw = {}
 
-        def load_a(b, g, offset):
-            raw[b, g] = shared.tile([P, PACK, PASS], F32, name="raw%d%d" % (b, g), align_bytes=64, offset=offset)
+        def load_a(b, g, s, offset):
+            raw[b, g, s] = placed([P, PACK, SIDE], F32, "raw%d%d%d" % (b, g, s), offset)
+            col = b * PASS + s * SIDE
             nc.sync.dma_start(
-                raw[b, g][:],
-                a[g * PASS : (g + 1) * PASS, b * PASS : (b + 1) * PASS].rearrange("(p j) c -> p j c", j=PACK),
+                raw[b, g, s][:],
+                a[g * PASS : (g + 1) * PASS, col : col + SIDE].rearrange("(p j) c -> p j c", j=PACK),
             )
 
-        load_a(0, 0, 2 * RAW_BYTES)
-        drift = keep.tile([P, 2, PACK], F32, name="drift")
-        nc.sync.dma_start(drift[:], d.rearrange("(b p t) -> p b t", b=2, t=PACK))
+        load_a(0, 0, 0, 5 * RAW)
+        load_a(0, 0, 1, 6 * RAW)
 
         v_scales = []
         for g in range(2):
-            rows = keep.tile([P, S // 4], I32, name="v_scales%d" % g, align_bytes=64)
+            rows = sbuf([P, S // 4], I32, "v_scales%d" % g)
             nc.vector.memset(rows[:], 0)
-            v_scales.append(rows)
-        picked_scales = keep.tile([P, S], U8, name="picked_scales", align_bytes=64)
+            v_scales.append(rows[:].bitcast(U8))
+        picked_scales = sbuf([P, S], U8, "picked_scales")
         nc.vector.tensor_copy(picked_scales[:], scale_window[:].indirect(offsets[:]))
 
         def place_scales(g):
             for quad in range(4):
                 row = SCALE_ROWS + 16 * g + 4 * quad
                 nc.sync.dma_start(
-                    v_scales[g][32 * quad : 32 * quad + 4, :], picked_scales[row : row + 4, :].bitcast(I32)
+                    v_scales[g][32 * quad : 32 * quad + 4, :].bitcast(I32), picked_scales[row : row + 4, :].bitcast(I32)
                 )
 
         place_scales(0)
-        load_a(0, 1, 0)
+        load_a(0, 1, 0, 0)
+        load_a(0, 1, 1, RAW + T // 4)
         place_scales(1)
-        load_a(1, 0, RAW_BYTES)
+        drift = placed([P, 2, PACK], F32, "drift", RAW)
+        nc.sync.dma_start(drift[:], d.rearrange("(b p t) -> p b t", b=2, t=PACK))
 
-        v_words = []
-        for half in range(2):
-            picked = keep.tile([P, HALF], U32, name="picked%d" % half, align_bytes=64)
+        picked, v_words = {}, {}
+
+        def pick(half, offset):
+            picked[half] = placed([P, HALF], U32, "picked%d" % half, offset)
             columns = slice(half * HALF // 16, (half + 1) * HALF // 16)
-            nc.vector.tensor_copy(picked[:], word_window[:].bitcast(U32).indirect(offsets[:, columns]))
-            parted = keep.tile([P, 2, HALF], U16, name="parted%d" % half, align_bytes=64)
-            both = picked[:].bitcast(U16).rearrange("p (n g) -> p g n", g=2)
-            for g in range(2):
-                nc.vector.tensor_copy(parted[:, g, :], both[:, g, :])
-            v_words.append(parted)
+            nc.vector.tensor_copy(picked[half][:], word_window[:].bitcast(U32).indirect(offsets[:, columns]))
 
-        a_codes, a_scales = {}, {}
+        def part(half, on=None):
+            v_words[half] = sbuf([P, 2, HALF], U16, "parted%d" % half, on)
+            both = picked[half][:].bitcast(U16).rearrange("p (n g) -> p g n", g=2)
+            nc.vector.tensor_copy(v_words[half][:], both)
 
-        def quantize_a(b, g):
-            src = raw[b, g][:].rearrange("p j (m u t) -> p u m j t", u=2, t=2)
+        pick(0, 7 * RAW)
+        part(0)
+        pick(1, 8 * RAW)
+        load_a(1, 0, 0, 7 * RAW)
+        load_a(1, 0, 1, 3 * RAW)
+        load_a(1, 1, 0, 4 * RAW)
+
+        a_codes, a_scales, grouped = {}, {}, {}
+
+        def copy_on(engine, dst, src):
+            if engine == "v":
+                nc.vector.tensor_copy(dst, src)
+            else:
+                nc.scalar.copy(dst, src)
+
+        def round_a(b, g, s, engine):
+            if (b, g) not in grouped:
+                grouped[b, g] = sbuf([P, PACK, P, PACK], BF16, "grouped%d%d" % (b, g))
+            src = raw[b, g, s][:].rearrange("p j (m t) -> p m j t", t=PACK)
+            dst = grouped[b, g][:, :, s * P // 2 : (s + 1) * P // 2, :].rearrange("p t m j -> p m j t")
+            copy_on(engine, dst, src)
+
+        def quantize_a(b, g, u, source):
+            name = "%d%d%d" % (b, g, u)
+            codes = sbuf([P, 2 * P], U32, "a_codes" + name)
+            scales = sbuf([P, 2 * P], U8, "a_scales" + name)
+            nc.vector.quantize_mx(out=codes[:].bitcast(FP8X4), scales=scales[:], in_=source)
+            for t in range(2):
+                a_codes[b, g, 2 * u + t] = codes[:, t * P : (t + 1) * P]
+                a_scales[b, g, 2 * u + t] = scales[:, t * P : (t + 1) * P]
+
+        def quantize_part(b, g):
             for u in range(2):
-                name = "%d%d%d" % (b, g, u)
-                grouped = keep.tile([P, 2 * PASS], BF16, name="grouped" + name, tag="grouped" + name, align_bytes=64)
-                dst = grouped[:].rearrange("p (t m j) -> p m j t", t=2, j=PACK)
-                if (b, g, u) in ROUNDED_ON_VECTOR:
-                    nc.vector.tensor_copy(dst, src[:, u])
-                else:
-                    nc.scalar.copy(dst, src[:, u])
-                codes = keep.tile([P, 2 * P], U32, name="a_codes" + name, align_bytes=64)
-                scales = keep.tile([P, 2 * P], U8, name="a_scales" + name, align_bytes=64)
-                nc.vector.quantize_mx(out=codes[:].bitcast(FP8X4), scales=scales[:], in_=grouped[:])
-                for t in range(2):
-                    a_codes[b, g, 2 * u + t] = codes[:, t * P : (t + 1) * P]
-                    a_scales[b, g, 2 * u + t] = scales[:, t * P : (t + 1) * P]
+                quantize_a(b, g, u, grouped[b, g][:, 2 * u : 2 * u + 2].rearrange("p t m j -> p (t m j)"))
 
-        quantize_a(0, 0)
-        load_a(1, 1, 2 * RAW_BYTES)
-        quantize_a(0, 1)
+        def round_pair(b, g, s, u, engine):
+            if (b, g, u) not in grouped:
+                grouped[b, g, u] = sbuf([P, 2, P, PACK], BF16, "grouped%d%d%d" % (b, g, u))
+            src = raw[b, g, s][:].rearrange("p j (m u t) -> p u m j t", u=2, t=2)[:, u]
+            dst = grouped[b, g, u][:, :, s * P // 2 : (s + 1) * P // 2, :].rearrange("p t m j -> p m j t")
+            copy_on(engine, dst, src)
 
-        c_words = shared.tile([P, 2, N // 2], I32, name="c_words", align_bytes=64, offset=0)
+        def quantize_pair(b, g, u):
+            quantize_a(b, g, u, grouped[b, g, u][:].rearrange("p t m j -> p (t m j)"))
+
+        for s in range(2):
+            for u in range(2):
+                round_pair(0, 0, s, u, "s")
+        quantize_pair(0, 0, 0)
+        part(1, "grouped000")
+        quantize_pair(0, 0, 1)
+        load_a(1, 1, 1, 5 * RAW)
+
+        for s in range(2):
+            round_pair(0, 1, s, 0, "v")
+            round_pair(0, 1, s, 1, "s")
+        quantize_pair(0, 1, 0)
+        quantize_pair(0, 1, 1)
+
+        c_words = placed([P, 2, N // 2], I32, "c_words", 0)
         nc.sync.dma_start(c_words[:], c4_words.rearrange("b p x -> p b x").bitcast(I32))
-        weight = shared.tile([P, N // P], F32, name="weight", align_bytes=64, offset=3072)
-        setpoint = shared.tile([P, N // P], F32, name="setpoint", align_bytes=64, offset=3136)
-        with nc.allow_non_contiguous_dma(reason="one value a partition"):
-            nc.sync.dma_start(weight[:], q.rearrange("(c p) -> p c", p=P))
-            nc.sync.dma_start(setpoint[:], r.rearrange("(c p) -> p c", p=P))
-        c_scales = shared.tile([P, 2, N // 4], I32, name="c_scales", align_bytes=64, offset=2048)
+        c_scales = placed([P, 2, N // 4], I32, "c_scales", 2048)
         nc.gpsimd.memset(c_scales[:], 0)
         for quad in range(4):
             nc.sync.dma_start(
                 c_scales[32 * quad : 32 * quad + 4, :, :],
                 c4_scales[:, 4 * quad : 4 * quad + 4, :].rearrange("b m c -> m b c").bitcast(I32),
             )
+        weight = placed([P, N // P], F32, "weight", 3072)
+        setpoint = placed([P, N // P], F32, "setpoint", 3136)
+        with nc.allow_non_contiguous_dma(reason="one value a partition"):
+            nc.sync.dma_start(weight[:], q.rearrange("(c p) -> p c", p=P))
+            nc.sync.dma_start(setpoint[:], r.rearrange("(c p) -> p c", p=P))
 
         exponent = keep.tile([P, N // P], F32, name="exponent")
         root = keep.tile([P, N // P], F32, name="root")
@@ -141,50 +186,57 @@ def tile_list_logged_state_cost_kernel(tc, tab, offs, a, d, c4_words, c4_scales,
         nc.gpsimd.tensor_tensor(scaled[:], setpoint[:], root[:], ALU.mult)
         nc.gpsimd.tensor_scalar(shift[:], scaled[:], -1.0, 0.0, ALU.mult, ALU.add)
 
-        quantize_a(1, 0)
-        quantize_a(1, 1)
+        round_a(1, 0, 0, "s")
+        round_a(1, 0, 1, "s")
+        quantize_part(1, 0)
+        for s in range(2):
+            round_pair(1, 1, s, 0, "v")
+            round_pair(1, 1, s, 1, "s")
+        quantize_pair(1, 1, 0)
+        quantize_pair(1, 1, 1)
 
-        def first_pass(sums, b, g, t, first, width, start, stop):
-            half, col = divmod(first, HALF)
+        def first_pass(sums, b, g, t, token, width, start, stop):
+            half, col = divmod(token, HALF)
             nc.tensor.matmul_mx(
                 out=sums,
                 lhsT=a_codes[b, g, t].bitcast(FP8X4),
                 lhsT_scale=a_scales[b, g, t],
                 rhs=v_words[half][:, g, col : col + width].bitcast(FP4X4),
-                rhs_scale=v_scales[g][:].bitcast(U8)[:, first : first + width],
+                rhs_scale=v_scales[g][:, token : token + width],
                 start=start,
                 stop=stop,
             )
 
-        def narrow_product(b):
-            banks = [psum.tile([P, PACK, CHUNK], F32, name="bank", tag="bank") for chunk in range(HALF // CHUNK)]
-            for chunk, bank in enumerate(banks):
+        def narrow_product(b, bank0):
+            banks = [bank([P, PACK, CHUNK], bank0 + chunk) for chunk in range(HALF // CHUNK)]
+            for chunk, sums in enumerate(banks):
                 for g in range(2):
                     for t in range(PACK):
                         start, stop = (g, t) == (0, 0), (g, t) == (1, PACK - 1)
-                        first_pass(bank[:, t, :], b, g, t, chunk * CHUNK, CHUNK, start, stop)
+                        first_pass(sums[:, t, :], b, g, t, chunk * CHUNK, CHUNK, start, stop)
             return banks
 
-        def wide_product(b):
-            banks = [psum.tile([P, HALF], F32, name="bank", tag="bank") for t in range(PACK)]
-            for t, bank in enumerate(banks):
-                for g in range(2):
-                    first_pass(bank[:], b, g, t, HALF, HALF, g == 0, g == 1)
+        def wide_product(b, bank0, order):
+            banks = [bank([P, HALF], bank0 + t) for t in range(PACK)]
+            for t, sums in enumerate(banks):
+                for g in order:
+                    first_pass(sums[:], b, g, t, HALF, HALF, g == order[0], g == order[1])
             return banks
 
-        h_codes, h_scales = {}, {}
+        h_codes = {(b, half): sbuf([P, HALF], U32, "h_codes%d%d" % (b, half)) for b, half in ((0, 1), (1, 0), (1, 1))}
+        h_codes[0, 0] = placed([P, HALF], U32, "h_codes00", 5 * RAW)
+        h_scales = {(b, half): sbuf([P, HALF], U8, "h_scales%d%d" % (b, half)) for b in range(2) for half in range(2)}
 
         def quantize_h(b, piece, rounded):
-            h_codes[b, piece] = keep.tile([P, PIECE], U32, name="h_codes%d%d" % (b, piece), align_bytes=64)
-            h_scales[b, piece] = keep.tile([P, PIECE], U8, name="h_scales%d%d" % (b, piece), align_bytes=64)
+            half, col = divmod(piece * PIECE, HALF)
             nc.vector.quantize_mx(
-                out=h_codes[b, piece][:].bitcast(FP8X4),
-                scales=h_scales[b, piece][:],
+                out=h_codes[b, half][:, col : col + PIECE].bitcast(FP8X4),
+                scales=h_scales[b, half][:, col : col + PIECE],
                 in_=rounded[:].rearrange("p n t -> p (n t)"),
             )
 
-        def narrow_finish(b, piece, banks, tag):
-            rounded = keep.tile([P, PIECE, PACK], BF16, name="rounded", tag=tag, align_bytes=64)
+        def narrow_drain(b, piece, banks):
+            rounded = sbuf([P, PIECE, PACK], BF16, "rounded%d%d" % (b, piece))
             for u in range(2):
                 nc.vector.tensor_tensor(
                     rounded[:, u * CHUNK : (u + 1) * CHUNK, :],
@@ -192,69 +244,80 @@ def tile_list_logged_state_cost_kernel(tc, tab, offs, a, d, c4_words, c4_scales,
                     drift[:, b : b + 1, :].to_broadcast([P, CHUNK, PACK]),
                     ALU.add,
                 )
-            quantize_h(b, piece, rounded)
+            return rounded
 
         def wide_drain(b, banks, offset):
-            tiles = shared.tile([P, PACK, HALF], BF16, name="tiles%d" % b, align_bytes=64, offset=offset)
+            tiles = placed([P, PACK, HALF], BF16, "tiles%d" % b, offset)
             for t in range(PACK):
                 nc.scalar.activation(tiles[:, t, :], banks[t][:], ACT.Identity, bias=drift[:, b, t : t + 1])
             return tiles
 
-        def wide_finish(b, piece, tiles):
-            rounded = keep.tile([P, PIECE, PACK], BF16, name="rounded%d%d" % (b, piece), align_bytes=64)
+        def interleave(b, piece, tiles, engine):
+            rounded = sbuf([P, PIECE, PACK], BF16, "rounded%d%d" % (b, piece))
             col = piece * PIECE - HALF
             dst = rounded[:].rearrange("p (c i) t -> p c t i", i=4)
             src = tiles[:, :, col : col + PIECE].rearrange("p t (c i) -> p c t i", i=4)
-            if b == INTERLEAVED_ON_SCALAR:
-                nc.scalar.copy(dst, src)
-            else:
-                nc.vector.tensor_copy(dst, src)
-            quantize_h(b, piece, rounded)
+            copy_on(engine, dst, src)
+            return rounded
 
-        def second_product(piece, on_vector):
-            banks = [psum.tile([P, 2, PIECE], F32, name="bank", tag="bank") for pair in range(2)]
-            for pair, bank in enumerate(banks):
+        def second_pass(sums, b, c, token, width, start, stop):
+            half, col = divmod(token, HALF)
+            nc.tensor.matmul_mx(
+                out=sums,
+                lhsT=c_words[:, b, c * P // 2 : (c + 1) * P // 2].bitcast(FP4X4),
+                lhsT_scale=c_scales[:, b, c * P // 4 : (c + 1) * P // 4].bitcast(U8),
+                rhs=h_codes[b, half][:, col : col + width].bitcast(FP8X4),
+                rhs_scale=h_scales[b, half][:, col : col + width],
+                start=start,
+                stop=stop,
+            )
+
+        def finish(sums, c, token, width, engine):
+            cost = keep.tile([P, width], F32, name="cost%d_%d" % (token, c))
+            if engine == "v":
+                deviation = keep.tile([P, width], F32, name="deviation%d_%d" % (token, c))
+                nc.vector.tensor_scalar(deviation[:], sums, root[:, c : c + 1], shift[:, c : c + 1], ALU.mult, ALU.add)
+                nc.vector.tensor_tensor(cost[:], deviation[:], deviation[:], ALU.mult)
+            else:
+                nc.scalar.activation(cost[:], sums, ACT.Square, bias=shift[:, c : c + 1], scale=root[:, c : c + 1])
+            nc.sync.dma_start(out[c * P : (c + 1) * P, token : token + width], cost[:])
+
+        def second_product(half, bank0, engines):
+            banks = [bank([P, HALF], bank0 + c) for c in range(N // P)]
+            for c, sums in enumerate(banks):
+                for b in range(2):
+                    second_pass(sums[:], b, c, half * HALF, HALF, b == 0, b == 1)
+            for c, sums in enumerate(banks):
+                finish(sums[:], c, half * HALF, HALF, engines[c])
+
+        def narrow_second(piece, bank0, engines):
+            banks = [bank([P, 2, PIECE], bank0 + pair) for pair in range(2)]
+            for pair, sums in enumerate(banks):
                 for b in range(2):
                     for u in range(2):
-                        c = 2 * pair + u
                         for col in range(0, PIECE, CHUNK):
-                            nc.tensor.matmul_mx(
-                                out=bank[:, u, col : col + CHUNK],
-                                lhsT=c_words[:, b, c * P // 2 : (c + 1) * P // 2].bitcast(FP4X4),
-                                lhsT_scale=c_scales[:, b, c * P // 4 : (c + 1) * P // 4].bitcast(U8),
-                                rhs=h_codes[b, piece][:, col : col + CHUNK].bitcast(FP8X4),
-                                rhs_scale=h_scales[b, piece][:, col : col + CHUNK],
-                                start=(b, u, col) == (0, 0, 0),
-                                stop=(b, u, col) == (1, 1, PIECE - CHUNK),
-                            )
+                            start, stop = (b, u, col) == (0, 0, 0), (b, u, col) == (1, 1, PIECE - CHUNK)
+                            second_pass(sums[:, u, col : col + CHUNK], b, 2 * pair + u, piece * PIECE + col, CHUNK, start, stop)
             for c in range(N // P):
-                sums = banks[c // 2][:, c % 2, :]
-                cost = keep.tile([P, PIECE], F32, name="cost%d%d" % (piece, c))
-                if c in on_vector:
-                    deviation = keep.tile([P, PIECE], F32, name="deviation%d" % c)
-                    nc.vector.tensor_scalar(
-                        deviation[:], sums, root[:, c : c + 1], shift[:, c : c + 1], ALU.mult, ALU.add
-                    )
-                    nc.vector.tensor_tensor(cost[:], deviation[:], deviation[:], ALU.mult)
-                else:
-                    nc.scalar.activation(cost[:], sums, ACT.Square, bias=shift[:, c : c + 1], scale=root[:, c : c + 1])
-                nc.sync.dma_start(out[c * P : (c + 1) * P, piece * PIECE : (piece + 1) * PIECE], cost[:])
+                finish(banks[c // 2][:, c % 2, :], c, piece * PIECE, PIECE, engines[c])
 
-        narrow0 = narrow_product(0)
-        wide0 = wide_product(0)
-        narrow_finish(0, 0, narrow0, "rounded00")
-        narrow1 = narrow_product(1)
-        tiles0 = wide_drain(0, wide0, 3 * RAW_BYTES // 2)
-        narrow_finish(1, 0, narrow1, "rounded10")
-        narrow_finish(0, 1, narrow0, "grouped111")
-        wide1 = wide_product(1)
-        wide_finish(0, 2, tiles0)
-        wide_finish(0, 3, tiles0)
-        tiles1 = wide_drain(1, wide1, 2 * RAW_BYTES)
-        second_product(0, ())
-        narrow_finish(1, 1, narrow1, "rounded11")
-        second_product(1, ())
-        wide_finish(1, 2, tiles1)
-        second_product(2, ())
-        wide_finish(1, 3, tiles1)
-        second_product(3, (0, 1))
+        narrow0 = narrow_product(0, 0)
+        wide0 = wide_product(0, 4, (1, 0))
+        rounded0 = [narrow_drain(0, piece, narrow0) for piece in range(2)]
+        tiles0 = wide_drain(0, wide0, 3 * RAW)
+        rounded02 = interleave(0, 2, tiles0, "s")
+        narrow1 = narrow_product(1, 0)
+        wide1 = wide_product(1, 4, (1, 0))
+        for piece in range(2):
+            quantize_h(0, piece, rounded0[piece])
+        rounded1 = [narrow_drain(1, piece, narrow1) for piece in range(2)]
+        tiles1 = wide_drain(1, wide1, 9 * RAW)
+        for piece in range(2):
+            quantize_h(1, piece, rounded1[piece])
+        second_product(0, 0, "ssss")
+        quantize_h(0, 2, rounded02)
+        quantize_h(0, 3, interleave(0, 3, tiles0, "v"))
+        for piece in (2, 3):
+            quantize_h(1, piece, interleave(1, piece, tiles1, "v"))
+        narrow_second(2, 4, "ssss")
+        narrow_second(3, 6, "vvss")

@@ -24,6 +24,7 @@ CHUNK = HALF // PACK
 PIECE = 2 * CHUNK
 SIDE = PASS // 2
 SCALE_ROWS = 96
+TAIL = ((512, 256, (4, 5), "ss"), (768, 128, (6, 0), "vs"), (896, 128, (7, 1), "vs"))
 RAW = PACK * SIDE * 4
 
 
@@ -98,15 +99,15 @@ def tile_list_logged_state_cost_kernel(tc, tab, offs, a, d, c4_words, c4_scales,
             columns = slice(half * HALF // 16, (half + 1) * HALF // 16)
             nc.vector.tensor_copy(picked[half][:], word_window[:].bitcast(U32).indirect(offsets[:, columns]))
 
-        def part(half, on=None):
-            v_words[half] = sbuf([P, 2, HALF], U16, "parted%d" % half, on)
+        def part(half, offset):
+            v_words[half] = placed([P, 2, HALF], U16, "parted%d" % half, offset)
             both = picked[half][:].bitcast(U16).rearrange("p (n g) -> p g n", g=2)
             nc.vector.tensor_copy(v_words[half][:], both)
 
-        pick(0, 7 * RAW)
-        part(0)
-        pick(1, 8 * RAW)
-        load_a(1, 0, 0, 7 * RAW)
+        pick(0, 8 * RAW - 1024)
+        part(0, 11 * RAW)
+        pick(1, 8 * RAW - 2048)
+        load_a(1, 0, 0, 8 * RAW)
         load_a(1, 0, 1, 3 * RAW)
         load_a(1, 1, 0, 4 * RAW)
 
@@ -152,7 +153,6 @@ def tile_list_logged_state_cost_kernel(tc, tab, offs, a, d, c4_words, c4_scales,
             for u in range(2):
                 round_pair(0, 0, s, u, "s")
         quantize_pair(0, 0, 0)
-        part(1, "grouped000")
         quantize_pair(0, 0, 1)
         load_a(1, 1, 1, 5 * RAW)
 
@@ -161,6 +161,7 @@ def tile_list_logged_state_cost_kernel(tc, tab, offs, a, d, c4_words, c4_scales,
             round_pair(0, 1, s, 1, "s")
         quantize_pair(0, 1, 0)
         quantize_pair(0, 1, 1)
+        part(1, RAW + 2048)
 
         c_words = placed([P, 2, N // 2], I32, "c_words", 0)
         nc.sync.dma_start(c_words[:], c4_words.rearrange("b p x -> p b x").bitcast(I32))
@@ -209,11 +210,13 @@ def tile_list_logged_state_cost_kernel(tc, tab, offs, a, d, c4_words, c4_scales,
 
         def narrow_product(b, bank0):
             banks = [bank([P, PACK, CHUNK], bank0 + chunk) for chunk in range(HALF // CHUNK)]
+            for u in range(2):
+                for chunk, sums in enumerate(banks):
+                    for t in (2 * u, 2 * u + 1):
+                        first_pass(sums[:, t, :], b, 0, t, chunk * CHUNK, CHUNK, t == 0, False)
             for chunk, sums in enumerate(banks):
-                for g in range(2):
-                    for t in range(PACK):
-                        start, stop = (g, t) == (0, 0), (g, t) == (1, PACK - 1)
-                        first_pass(sums[:, t, :], b, g, t, chunk * CHUNK, CHUNK, start, stop)
+                for t in range(PACK):
+                    first_pass(sums[:, t, :], b, 1, t, chunk * CHUNK, CHUNK, False, t == PACK - 1)
             return banks
 
         def wide_product(b, bank0, order):
@@ -227,11 +230,12 @@ def tile_list_logged_state_cost_kernel(tc, tab, offs, a, d, c4_words, c4_scales,
         h_codes[0, 0] = placed([P, HALF], U32, "h_codes00", 5 * RAW)
         h_scales = {(b, half): sbuf([P, HALF], U8, "h_scales%d%d" % (b, half)) for b in range(2) for half in range(2)}
 
-        def quantize_h(b, piece, rounded):
-            half, col = divmod(piece * PIECE, HALF)
+        def quantize_h(b, token, rounded):
+            half, col = divmod(token, HALF)
+            width = rounded.shape[1]
             nc.vector.quantize_mx(
-                out=h_codes[b, half][:, col : col + PIECE].bitcast(FP8X4),
-                scales=h_scales[b, half][:, col : col + PIECE],
+                out=h_codes[b, half][:, col : col + width].bitcast(FP8X4),
+                scales=h_scales[b, half][:, col : col + width],
                 in_=rounded[:].rearrange("p n t -> p (n t)"),
             )
 
@@ -252,11 +256,11 @@ def tile_list_logged_state_cost_kernel(tc, tab, offs, a, d, c4_words, c4_scales,
                 nc.scalar.activation(tiles[:, t, :], banks[t][:], ACT.Identity, bias=drift[:, b, t : t + 1])
             return tiles
 
-        def interleave(b, piece, tiles, engine):
-            rounded = sbuf([P, PIECE, PACK], BF16, "rounded%d%d" % (b, piece))
-            col = piece * PIECE - HALF
+        def interleave(b, token, width, tiles, engine, on=None):
+            rounded = sbuf([P, width, PACK], BF16, "woven%d_%d" % (b, token), on)
+            col = token - HALF
             dst = rounded[:].rearrange("p (c i) t -> p c t i", i=4)
-            src = tiles[:, :, col : col + PIECE].rearrange("p t (c i) -> p c t i", i=4)
+            src = tiles[:, :, col : col + width].rearrange("p t (c i) -> p c t i", i=4)
             copy_on(engine, dst, src)
             return rounded
 
@@ -272,52 +276,64 @@ def tile_list_logged_state_cost_kernel(tc, tab, offs, a, d, c4_words, c4_scales,
                 stop=stop,
             )
 
-        def finish(sums, c, token, width, engine):
-            cost = keep.tile([P, width], F32, name="cost%d_%d" % (token, c))
+        def finish(sums, first, token, engine):
+            count, width = sums.shape[1], sums.shape[2]
+            cost = keep.tile([P, count, width], F32, name="cost%d_%d" % (token, first))
             if engine == "v":
-                deviation = keep.tile([P, width], F32, name="deviation%d_%d" % (token, c))
-                nc.vector.tensor_scalar(deviation[:], sums, root[:, c : c + 1], shift[:, c : c + 1], ALU.mult, ALU.add)
+                deviation = keep.tile([P, count, width], F32, name="deviation%d_%d" % (token, first))
+                for u in range(count):
+                    c = first + u
+                    nc.vector.tensor_scalar(
+                        deviation[:, u, :], sums[:, u, :], root[:, c : c + 1], shift[:, c : c + 1], ALU.mult, ALU.add
+                    )
                 nc.vector.tensor_tensor(cost[:], deviation[:], deviation[:], ALU.mult)
             else:
-                nc.scalar.activation(cost[:], sums, ACT.Square, bias=shift[:, c : c + 1], scale=root[:, c : c + 1])
-            nc.sync.dma_start(out[c * P : (c + 1) * P, token : token + width], cost[:])
+                for u in range(count):
+                    c = first + u
+                    nc.scalar.activation(
+                        cost[:, u, :], sums[:, u, :], ACT.Square, bias=shift[:, c : c + 1], scale=root[:, c : c + 1]
+                    )
+            rows = out[first * P : (first + count) * P, token : token + width]
+            nc.sync.dma_start(rows.rearrange("(u p) n -> p u n", p=P), cost[:])
 
         def second_product(half, bank0, engines):
-            banks = [bank([P, HALF], bank0 + c) for c in range(N // P)]
+            banks = [bank([P, 1, HALF], bank0 + c) for c in range(N // P)]
             for c, sums in enumerate(banks):
                 for b in range(2):
-                    second_pass(sums[:], b, c, half * HALF, HALF, b == 0, b == 1)
+                    second_pass(sums[:, 0, :], b, c, half * HALF, HALF, b == 0, b == 1)
             for c, sums in enumerate(banks):
-                finish(sums[:], c, half * HALF, HALF, engines[c])
+                finish(sums[:], c, half * HALF, engines[c])
 
-        def narrow_second(piece, bank0, engines):
-            banks = [bank([P, 2, PIECE], bank0 + pair) for pair in range(2)]
-            for pair, sums in enumerate(banks):
+        def narrow_second(token, width, numbers, engines):
+            share = N // P // len(numbers)
+            banks = [bank([P, share, width], number) for number in numbers]
+            for x, sums in enumerate(banks):
                 for b in range(2):
-                    for u in range(2):
-                        for col in range(0, PIECE, CHUNK):
-                            start, stop = (b, u, col) == (0, 0, 0), (b, u, col) == (1, 1, PIECE - CHUNK)
-                            second_pass(sums[:, u, col : col + CHUNK], b, 2 * pair + u, piece * PIECE + col, CHUNK, start, stop)
-            for c in range(N // P):
-                finish(banks[c // 2][:, c % 2, :], c, piece * PIECE, PIECE, engines[c])
+                    for u in range(share):
+                        for col in range(0, width, CHUNK):
+                            start, stop = (b, u, col) == (0, 0, 0), (b, u, col) == (1, share - 1, width - CHUNK)
+                            second_pass(sums[:, u, col : col + CHUNK], b, share * x + u, token + col, CHUNK, start, stop)
+            count = PIECE // width
+            for c in range(0, N // P, count):
+                x, u = divmod(c, share)
+                finish(banks[x][:, u : u + count, :], c, token, engines[x])
 
         narrow0 = narrow_product(0, 0)
         wide0 = wide_product(0, 4, (1, 0))
         rounded0 = [narrow_drain(0, piece, narrow0) for piece in range(2)]
-        tiles0 = wide_drain(0, wide0, 3 * RAW)
-        rounded02 = interleave(0, 2, tiles0, "s")
+        tiles0 = wide_drain(0, wide0, 5 * RAW + 2048)
         narrow1 = narrow_product(1, 0)
         wide1 = wide_product(1, 4, (1, 0))
         for piece in range(2):
-            quantize_h(0, piece, rounded0[piece])
+            quantize_h(0, piece * PIECE, rounded0[piece])
         rounded1 = [narrow_drain(1, piece, narrow1) for piece in range(2)]
-        tiles1 = wide_drain(1, wide1, 9 * RAW)
+        tiles1 = wide_drain(1, wide1, 10 * RAW)
         for piece in range(2):
-            quantize_h(1, piece, rounded1[piece])
+            quantize_h(1, piece * PIECE, rounded1[piece])
         second_product(0, 0, "ssss")
-        quantize_h(0, 2, rounded02)
-        quantize_h(0, 3, interleave(0, 3, tiles0, "v"))
-        for piece in (2, 3):
-            quantize_h(1, piece, interleave(1, piece, tiles1, "v"))
-        narrow_second(2, 4, "ssss")
-        narrow_second(3, 6, "vvss")
+        for token, width, numbers, engines in TAIL:
+            early = interleave(0, token, width, tiles0, "v")
+            late = interleave(1, token, width, tiles1, "v")
+            quantize_h(0, token, early)
+            quantize_h(1, token, late)
+            narrow_second(token, width, numbers, engines)

@@ -24,7 +24,9 @@ CHUNK = HALF // PACK
 PIECE = 2 * CHUNK
 SIDE = PASS // 2
 SCALE_ROWS = 96
-TAIL = ((512, 256, (4, 5), "ss"), (768, 128, (6, 0), "vs"), (896, 128, (7, 1), "vs"))
+TAIL = ((512, 256, ((4, 2, "s"), (5, 2, "s"))), (768, 128, ((6, 2, "v"), (0, 2, "s"))), (896, 128, ((7, 2, "v"), (1, 1, "s"), (2, 1, "s"))))
+SHARE = ("vs", "vs")
+WIDE = "ssss"
 RAW = PACK * SIDE * 4
 
 
@@ -191,8 +193,8 @@ def tile_list_logged_state_cost_kernel(tc, tab, offs, a, d, c4_words, c4_scales,
         round_a(1, 0, 1, "s")
         quantize_part(1, 0)
         for s in range(2):
-            round_pair(1, 1, s, 0, "v")
-            round_pair(1, 1, s, 1, "s")
+            for u in range(2):
+                round_pair(1, 1, s, u, SHARE[s][u])
         quantize_pair(1, 1, 0)
         quantize_pair(1, 1, 1)
 
@@ -304,19 +306,22 @@ def tile_list_logged_state_cost_kernel(tc, tab, offs, a, d, c4_words, c4_scales,
             for c, sums in enumerate(banks):
                 finish(sums[:], c, half * HALF, engines[c])
 
-        def narrow_second(token, width, numbers, engines):
-            share = N // P // len(numbers)
-            banks = [bank([P, share, width], number) for number in numbers]
-            for x, sums in enumerate(banks):
+        def narrow_second(token, width, plan):
+            first = 0
+            pending = []
+            for number, count, engine in plan:
+                sums = bank([P, count, width], number)
                 for b in range(2):
-                    for u in range(share):
+                    for u in range(count):
                         for col in range(0, width, CHUNK):
-                            start, stop = (b, u, col) == (0, 0, 0), (b, u, col) == (1, share - 1, width - CHUNK)
-                            second_pass(sums[:, u, col : col + CHUNK], b, share * x + u, token + col, CHUNK, start, stop)
-            count = PIECE // width
-            for c in range(0, N // P, count):
-                x, u = divmod(c, share)
-                finish(banks[x][:, u : u + count, :], c, token, engines[x])
+                            start, stop = (b, u, col) == (0, 0, 0), (b, u, col) == (1, count - 1, width - CHUNK)
+                            second_pass(sums[:, u, col : col + CHUNK], b, first + u, token + col, CHUNK, start, stop)
+                pending.append((sums, first, count, engine))
+                first = first + count
+            for sums, first, count, engine in pending:
+                step = 1 if width == PIECE else count
+                for u in range(0, count, step):
+                    finish(sums[:, u : u + step, :], first + u, token, engine)
 
         narrow0 = narrow_product(0, 0)
         wide0 = wide_product(0, 4, (1, 0))
@@ -330,10 +335,10 @@ def tile_list_logged_state_cost_kernel(tc, tab, offs, a, d, c4_words, c4_scales,
         tiles1 = wide_drain(1, wide1, 10 * RAW)
         for piece in range(2):
             quantize_h(1, piece * PIECE, rounded1[piece])
-        second_product(0, 0, "ssss")
-        for token, width, numbers, engines in TAIL:
+        second_product(0, 0, WIDE)
+        for token, width, plan in TAIL:
             early = interleave(0, token, width, tiles0, "v")
             late = interleave(1, token, width, tiles1, "v")
             quantize_h(0, token, early)
             quantize_h(1, token, late)
-            narrow_second(token, width, numbers, engines)
+            narrow_second(token, width, plan)

@@ -46,6 +46,11 @@ def tile_list_logged_state_cost_kernel(tc, tab, offs, a, d, c4_words, c4_scales,
         def bank(shape, number):
             return psum.tile(shape, F32, name="bank%d" % number, tag="bank%d" % number)
 
+        one = keep.tile([P, 1], F32, name="one")
+        unread = keep.tile([P, 1], F32, name="unread")
+        nc.gpsimd.memset(one[:], 1.0)
+        nc.scalar.activation(unread[:], one[:], ACT.Sqrt)
+
         offsets = keep.tile([P, S // 16], U16, name="offsets")
         nc.sync.dma_start(offsets[:], offs)
         scale_window = placed([P, T], U8, "scale_window", RAW - T // 4)
@@ -180,14 +185,8 @@ def tile_list_logged_state_cost_kernel(tc, tab, offs, a, d, c4_words, c4_scales,
             nc.sync.dma_start(weight[:], q.rearrange("(c p) -> p c", p=P))
             nc.sync.dma_start(setpoint[:], r.rearrange("(c p) -> p c", p=P))
 
-        exponent = keep.tile([P, N // P], F32, name="exponent")
         root = keep.tile([P, N // P], F32, name="root")
-        scaled = keep.tile([P, N // P], F32, name="scaled")
         shift = keep.tile([P, N // P], F32, name="shift")
-        nc.gpsimd.memset(exponent[:], 0.5)
-        nc.gpsimd.tensor_tensor(root[:], weight[:], exponent[:], ALU.pow)
-        nc.gpsimd.tensor_tensor(scaled[:], setpoint[:], root[:], ALU.mult)
-        nc.gpsimd.tensor_scalar(shift[:], scaled[:], -1.0, 0.0, ALU.mult, ALU.add)
 
         round_a(1, 0, 0, "s")
         round_a(1, 0, 1, "s")
@@ -332,6 +331,8 @@ def tile_list_logged_state_cost_kernel(tc, tab, offs, a, d, c4_words, c4_scales,
         for piece in range(2):
             quantize_h(0, piece * PIECE, rounded0[piece])
         rounded1 = [narrow_drain(1, piece, narrow1) for piece in range(2)]
+        nc.scalar.activation(root[:], weight[:], ACT.Sqrt)
+        nc.vector.scalar_tensor_tensor(shift[:], setpoint[:], -1.0, root[:], ALU.mult, ALU.mult)
         tiles1 = wide_drain(1, wide1, 10 * RAW)
         for piece in range(2):
             quantize_h(1, piece * PIECE, rounded1[piece])

@@ -24,8 +24,8 @@ CHUNK = HALF // PACK
 PIECE = 2 * CHUNK
 SIDE = PASS // 2
 SCALE_ROWS = 96
-TAIL = ((512, 256, ((4, 2, "s"), (5, 2, "s"))), (768, 128, ((6, 2, "v"), (0, 2, "s"))), (896, 128, ((7, 2, "v"), (1, 1, "s"), (2, 1, "s"))))
-SHARE = ("vs", "vs")
+TAIL = ((512, 256, ((4, 2, "s"), (5, 2, "s"))), (768, 128, ((6, 2, "v"), (0, 2, "s"))), (896, 128, ((7, 1, "v"), (1, 2, "s"), (2, 1, "s"))))
+SHARE = ("ss", "vv")
 WIDE = "ssss"
 RAW = PACK * SIDE * 4
 
@@ -48,7 +48,7 @@ def tile_list_logged_state_cost_kernel(tc, tab, offs, a, d, c4_words, c4_scales,
 
         one = keep.tile([P, 1], F32, name="one")
         unread = keep.tile([P, 1], F32, name="unread")
-        nc.gpsimd.memset(one[:], 1.0)
+        nc.vector.memset(one[:], 1.0)
         nc.scalar.activation(unread[:], one[:], ACT.Sqrt)
 
         offsets = keep.tile([P, S // 16], U16, name="offsets")
@@ -96,8 +96,13 @@ def tile_list_logged_state_cost_kernel(tc, tab, offs, a, d, c4_words, c4_scales,
         load_a(0, 1, 0, 0)
         load_a(0, 1, 1, RAW + T // 4)
         place_scales(1)
-        drift = placed([P, 2, PACK], F32, "drift", RAW)
-        nc.sync.dma_start(drift[:], d.rearrange("(b p t) -> p b t", b=2, t=PACK))
+        drift = {}
+
+        def load_drift(b, offset):
+            drift[b] = placed([P, 1, PACK], F32, "drift%d" % b, offset)
+            nc.sync.dma_start(drift[b][:, 0, :], d[b * PASS : (b + 1) * PASS].rearrange("(p t) -> p t", t=PACK))
+
+        load_drift(0, RAW)
 
         picked, v_words = {}, {}
 
@@ -170,10 +175,10 @@ def tile_list_logged_state_cost_kernel(tc, tab, offs, a, d, c4_words, c4_scales,
         quantize_pair(0, 1, 1)
         part(1, RAW + 2048)
 
+        load_drift(1, 3200)
         c_words = placed([P, 2, N // 2], I32, "c_words", 0)
         nc.sync.dma_start(c_words[:], c4_words.rearrange("b p x -> p b x").bitcast(I32))
         c_scales = placed([P, 2, N // 4], I32, "c_scales", 2048)
-        nc.gpsimd.memset(c_scales[:], 0)
         for quad in range(4):
             nc.sync.dma_start(
                 c_scales[32 * quad : 32 * quad + 4, :, :],
@@ -246,7 +251,7 @@ def tile_list_logged_state_cost_kernel(tc, tab, offs, a, d, c4_words, c4_scales,
                 nc.vector.tensor_tensor(
                     rounded[:, u * CHUNK : (u + 1) * CHUNK, :],
                     banks[2 * piece + u][:].rearrange("p t n -> p n t"),
-                    drift[:, b : b + 1, :].to_broadcast([P, CHUNK, PACK]),
+                    drift[b][:].to_broadcast([P, CHUNK, PACK]),
                     ALU.add,
                 )
             return rounded
@@ -254,7 +259,7 @@ def tile_list_logged_state_cost_kernel(tc, tab, offs, a, d, c4_words, c4_scales,
         def wide_drain(b, banks, offset):
             tiles = placed([P, PACK, HALF], BF16, "tiles%d" % b, offset)
             for t in range(PACK):
-                nc.scalar.activation(tiles[:, t, :], banks[t][:], ACT.Identity, bias=drift[:, b, t : t + 1])
+                nc.scalar.activation(tiles[:, t, :], banks[t][:], ACT.Identity, bias=drift[b][:, 0, t : t + 1])
             return tiles
 
         def interleave(b, token, width, tiles, engine, on=None):
@@ -312,9 +317,8 @@ def tile_list_logged_state_cost_kernel(tc, tab, offs, a, d, c4_words, c4_scales,
                 sums = bank([P, count, width], number)
                 for b in range(2):
                     for u in range(count):
-                        for col in range(0, width, CHUNK):
-                            start, stop = (b, u, col) == (0, 0, 0), (b, u, col) == (1, count - 1, width - CHUNK)
-                            second_pass(sums[:, u, col : col + CHUNK], b, first + u, token + col, CHUNK, start, stop)
+                        start, stop = (b, u) == (0, 0), (b, u) == (1, count - 1)
+                        second_pass(sums[:, u, :], b, first + u, token, width, start, stop)
                 pending.append((sums, first, count, engine))
                 first = first + count
             for sums, first, count, engine in pending:
@@ -325,7 +329,7 @@ def tile_list_logged_state_cost_kernel(tc, tab, offs, a, d, c4_words, c4_scales,
         narrow0 = narrow_product(0, 0)
         wide0 = wide_product(0, 4, (1, 0))
         rounded0 = [narrow_drain(0, piece, narrow0) for piece in range(2)]
-        tiles0 = wide_drain(0, wide0, 5 * RAW + 2048)
+        tiles0 = wide_drain(0, wide0, 4 * RAW)
         narrow1 = narrow_product(1, 0)
         wide1 = wide_product(1, 4, (1, 0))
         for piece in range(2):

@@ -24,7 +24,7 @@ CHUNK = HALF // PACK
 PIECE = 2 * CHUNK
 SIDE = PASS // 2
 SCALE_ROWS = 96
-TAIL = ((512, 256, ((4, 2, "s"), (5, 2, "s"))), (768, 128, ((6, 2, "v"), (0, 2, "s"))), (896, 128, ((7, 1, "v"), (1, 2, "s"), (2, 1, "s"))))
+TAIL = ((512, 256, ((4, 2, "s"), (5, 2, "s"))), (768, 128, ((6, 2, "v"), (0, 2, "s"))), (896, 128, ((7, 2, "v"), (1, 1, "s"), (2, 1, "s"))))
 SHARE = ("ss", "vv")
 WIDE = "ssss"
 RAW = PACK * SIDE * 4
@@ -175,6 +175,11 @@ def tile_list_logged_state_cost_kernel(tc, tab, offs, a, d, c4_words, c4_scales,
         quantize_pair(0, 1, 1)
         part(1, RAW + 2048)
 
+        rows = raw[0, 0, 1][:, 0, 0:P]
+        for first, values in enumerate((q, r)):
+            nc.sync.dma_start(
+                rows[first:P:32, :].rearrange("x (c j) -> x c j", j=32), values.rearrange("(c x j) -> x c j", x=4, j=32)
+            )
         load_drift(1, 3200)
         c_words = placed([P, 2, N // 2], I32, "c_words", 0)
         nc.sync.dma_start(c_words[:], c4_words.rearrange("b p x -> p b x").bitcast(I32))
@@ -184,11 +189,6 @@ def tile_list_logged_state_cost_kernel(tc, tab, offs, a, d, c4_words, c4_scales,
                 c_scales[32 * quad : 32 * quad + 4, :, :],
                 c4_scales[:, 4 * quad : 4 * quad + 4, :].rearrange("b m c -> m b c").bitcast(I32),
             )
-        weight = placed([P, N // P], F32, "weight", 3072)
-        setpoint = placed([P, N // P], F32, "setpoint", 3136)
-        with nc.allow_non_contiguous_dma(reason="one value a partition"):
-            nc.sync.dma_start(weight[:], q.rearrange("(c p) -> p c", p=P))
-            nc.sync.dma_start(setpoint[:], r.rearrange("(c p) -> p c", p=P))
 
         root = keep.tile([P, N // P], F32, name="root")
         shift = keep.tile([P, N // P], F32, name="shift")
@@ -334,9 +334,11 @@ def tile_list_logged_state_cost_kernel(tc, tab, offs, a, d, c4_words, c4_scales,
         wide1 = wide_product(1, 4, (1, 0))
         for piece in range(2):
             quantize_h(0, piece * PIECE, rounded0[piece])
+        turned = keep.tile([P, P], F32, name="turned", align_bytes=64)
+        nc.vector.transpose(turned[:], rows)
+        nc.scalar.activation(root[:], turned[:, 0:P:32], ACT.Sqrt)
         rounded1 = [narrow_drain(1, piece, narrow1) for piece in range(2)]
-        nc.scalar.activation(root[:], weight[:], ACT.Sqrt)
-        nc.vector.scalar_tensor_tensor(shift[:], setpoint[:], -1.0, root[:], ALU.mult, ALU.mult)
+        nc.vector.scalar_tensor_tensor(shift[:], turned[:, 1:P:32], -1.0, root[:], ALU.mult, ALU.mult)
         tiles1 = wide_drain(1, wide1, 10 * RAW)
         for piece in range(2):
             quantize_h(1, piece * PIECE, rounded1[piece])

from contextlib import ExitStack

import concourse.mybir as mybir

K, T, S, H, N = 1024, 2048, 1024, 1024, 512
FLOPS = 2 * K * H * S + 2 * H * N * S

F32 = mybir.dt.float32
BF16 = mybir.dt.bfloat16
I32 = mybir.dt.int32
U32 = mybir.dt.uint32
U16 = mybir.dt.uint16
U8 = mybir.dt.uint8
FP8X4 = mybir.dt.float8_e4m3fn_x4
FP4X4 = mybir.dt.float4_e2m1fn_x4
ALU = mybir.AluOpType
ACT = mybir.ActivationFunctionType

P = 128
PACK = 4
PASS = P * PACK
HALF = S // 2
CHUNK = HALF // PACK
PIECE = 2 * CHUNK
SIDE = PASS // 2
SCALE_ROWS = 96
TAIL = ((512, 256, ((4, 2, "s"), (5, 2, "s"))), (768, 128, ((6, 2, "v"), (0, 2, "s"))), (896, 128, ((7, 2, "v"), (1, 1, "s"), (2, 1, "s"))))
SHARE = ("ss", "vv")
WIDE = "ssss"
RAW = PACK * SIDE * 4


def tile_list_logged_state_cost_kernel(tc, tab, offs, a, d, c4_words, c4_scales, r, q, out):
    nc = tc.nc
    with ExitStack() as ctx:
        keep = ctx.enter_context(tc.tile_pool(name="keep", bufs=1))
        shared = ctx.enter_context(tc.tile_pool(name="shared", bufs=1))
        psum = ctx.enter_context(tc.psum_pool(name="psum", bufs=1))

        def sbuf(shape, dtype, name, on=None):
            return keep.tile(shape, dtype, name=name, tag=on or name, align_bytes=64)

        def placed(shape, dtype, name, offset):
            return shared.tile(shape, dtype, name=name, align_bytes=64, offset=offset)

        def bank(shape, number):
            return psum.tile(shape, F32, name="bank%d" % number, tag="bank%d" % number)

        one = keep.tile([P, 1], F32, name="one")
        unread = keep.tile([P, 1], F32, name="unread")
        nc.vector.memset(one[:], 1.0)
        nc.scalar.activation(unread[:], one[:], ACT.Sqrt)

        offsets = keep.tile([P, S // 16], U16, name="offsets")
        nc.sync.dma_start(offsets[:], offs)
        scale_window = placed([P, T], U8, "scale_window", RAW - T // 4)
        nc.sync.dma_start(
            scale_window[SCALE_ROWS:P, :].bitcast(I32),
            tab[0, 512 * T : 544 * T].rearrange("(x t) -> x t", t=T).bitcast(I32),
        )
        nc.vector.memset(scale_window[0:64, :].bitcast(I32), 0)
        nc.vector.memset(scale_window[64:SCALE_ROWS, :].bitcast(I32), 0)

        word_window = placed([P, T], I32, "word_window", 3 * RAW)
        nc.sync.dma_start(word_window[:], tab[0, 0 : 512 * T].rearrange("(p x) -> p x", p=P).bitcast(I32))

        raw = {}

        def load_a(b, g, s, offset):
            raw[b, g, s] = placed([P, PACK, SIDE], F32, "raw%d%d%d" % (b, g, s), offset)
            col = b * PASS + s * SIDE
            nc.sync.dma_start(
                raw[b, g, s][:],
                a[g * PASS : (g + 1) * PASS, col : col + SIDE].rearrange("(p j) c -> p j c", j=PACK),
            )

        load_a(0, 0, 0, 5 * RAW)
        load_a(0, 0, 1, 6 * RAW)

        v_scales = []
        for g in range(2):
            rows = sbuf([P, S // 4], I32, "v_scales%d" % g)
            nc.vector.memset(rows[:], 0)
            v_scales.append(rows[:].bitcast(U8))
        picked_scales = sbuf([P, S], U8, "picked_scales")
        nc.vector.tensor_copy(picked_scales[:], scale_window[:].indirect(offsets[:]))

        def place_scales(g):
            for quad in range(4):
                row = SCALE_ROWS + 16 * g + 4 * quad
                nc.sync.dma_start(
                    v_scales[g][32 * quad : 32 * quad + 4, :].bitcast(I32), picked_scales[row : row + 4, :].bitcast(I32)
                )

        place_scales(0)
        load_a(0, 1, 0, 0)
        load_a(0, 1, 1, RAW + T // 4)
        place_scales(1)
        drift = {}

        def load_drift(b, offset):
            drift[b] = placed([P, 1, PACK], F32, "drift%d" % b, offset)
            nc.sync.dma_start(drift[b][:, 0, :], d[b * PASS : (b + 1) * PASS].rearrange("(p t) -> p t", t=PACK))

        load_drift(0, RAW)

        picked, v_words = {}, {}

        def pick(half, offset):
            picked[half] = placed([P, HALF], U32, "picked%d" % half, offset)
            columns = slice(half * HALF // 16, (half + 1) * HALF // 16)
            nc.vector.tensor_copy(picked[half][:], word_window[:].bitcast(U32).indirect(offsets[:, columns]))

        def part(half, offset):
            v_words[half] = placed([P, 2, HALF], U16, "parted%d" % half, offset)
            both = picked[half][:].bitcast(U16).rearrange("p (n g) -> p g n", g=2)
            nc.vector.tensor_copy(v_words[half][:], both)

        pick(0, 8 * RAW - 1024)
        part(0, 11 * RAW)
        pick(1, 8 * RAW - 2048)
        load_a(1, 0, 0, 8 * RAW)
        load_a(1, 0, 1, 3 * RAW)
        load_a(1, 1, 0, 4 * RAW)

        a_codes, a_scales, grouped = {}, {}, {}

        def copy_on(engine, dst, src):
            if engine == "v":
                nc.vector.tensor_copy(dst, src)
            else:
                nc.scalar.copy(dst, src)

        def round_a(b, g, s, engine):
            if (b, g) not in grouped:
                grouped[b, g] = sbuf([P, PACK, P, PACK], BF16, "grouped%d%d" % (b, g))
            src = raw[b, g, s][:].rearrange("p j (m t) -> p m j t", t=PACK)
            dst = grouped[b, g][:, :, s * P // 2 : (s + 1) * P // 2, :].rearrange("p t m j -> p m j t")
            copy_on(engine, dst, src)

        def quantize_a(b, g, u, source):
            name = "%d%d%d" % (b, g, u)
            codes = sbuf([P, 2 * P], U32, "a_codes" + name)
            scales = sbuf([P, 2 * P], U8, "a_scales" + name)
            nc.vector.quantize_mx(out=codes[:].bitcast(FP8X4), scales=scales[:], in_=source)
            for t in range(2):
                a_codes[b, g, 2 * u + t] = codes[:, t * P : (t + 1) * P]
                a_scales[b, g, 2 * u + t] = scales[:, t * P : (t + 1) * P]

        def quantize_part(b, g):
            for u in range(2):
                quantize_a(b, g, u, grouped[b, g][:, 2 * u : 2 * u + 2].rearrange("p t m j -> p (t m j)"))

        def round_pair(b, g, s, u, engine):
            if (b, g, u) not in grouped:
                grouped[b, g, u] = sbuf([P, 2, P, PACK], BF16, "grouped%d%d%d" % (b, g, u))
            src = raw[b, g, s][:].rearrange("p j (m u t) -> p u m j t", u=2, t=2)[:, u]
            dst = grouped[b, g, u][:, :, s * P // 2 : (s + 1) * P // 2, :].rearrange("p t m j -> p m j t")
            copy_on(engine, dst, src)

        def quantize_pair(b, g, u):
            quantize_a(b, g, u, grouped[b, g, u][:].rearrange("p t m j -> p (t m j)"))

        for s in range(2):
            for u in range(2):
                round_pair(0, 0, s, u, "s")
        quantize_pair(0, 0, 0)
        quantize_pair(0, 0, 1)
        load_a(1, 1, 1, 5 * RAW)

        for s in range(2):
            round_pair(0, 1, s, 0, "v")
            round_pair(0, 1, s, 1, "s")
        quantize_pair(0, 1, 0)
        quantize_pair(0, 1, 1)
        part(1, RAW + 2048)

        rows = raw[0, 0, 1][:, 0, 0:P]
        for first, values in enumerate((q, r)):
            nc.sync.dma_start(
                rows[first:P:32, :].rearrange("x (c j) -> x c j", j=32), values.rearrange("(c x j) -> x c j", x=4, j=32)
            )
        load_drift(1, 3200)
        c_words = placed([P, 2, N // 2], I32, "c_words", 0)
        nc.sync.dma_start(c_words[:], c4_words.rearrange("b p x -> p b x").bitcast(I32))
        c_scales = placed([P, 2, N // 4], I32, "c_scales", 2048)
        for quad in range(4):
            nc.sync.dma_start(
                c_scales[32 * quad : 32 * quad + 4, :, :],
                c4_scales[:, 4 * quad : 4 * quad + 4, :].rearrange("b m c -> m b c").bitcast(I32),
            )

        root = keep.tile([P, N // P], F32, name="root")
        shift = keep.tile([P, N // P], F32, name="shift")

        round_a(1, 0, 0, "s")
        round_a(1, 0, 1, "s")
        quantize_part(1, 0)
        for s in range(2):
            for u in range(2):
                round_pair(1, 1, s, u, SHARE[s][u])
        quantize_pair(1, 1, 0)
        quantize_pair(1, 1, 1)

        def first_pass(sums, b, g, t, token, width, start, stop):
            half, col = divmod(token, HALF)
            nc.tensor.matmul_mx(
                out=sums,
                lhsT=a_codes[b, g, t].bitcast(FP8X4),
                lhsT_scale=a_scales[b, g, t],
                rhs=v_words[half][:, g, col : col + width].bitcast(FP4X4),
                rhs_scale=v_scales[g][:, token : token + width],
                start=start,
                stop=stop,
            )

        def narrow_product(b, bank0):
            banks = [bank([P, PACK, CHUNK], bank0 + chunk) for chunk in range(HALF // CHUNK)]
            for u in range(2):
                for chunk, sums in enumerate(banks):
                    for t in (2 * u, 2 * u + 1):
                        first_pass(sums[:, t, :], b, 0, t, chunk * CHUNK, CHUNK, t == 0, False)
            for chunk, sums in enumerate(banks):
                for t in range(PACK):
                    first_pass(sums[:, t, :], b, 1, t, chunk * CHUNK, CHUNK, False, t == PACK - 1)
            return banks

        def wide_product(b, bank0, order):
            banks = [bank([P, HALF], bank0 + t) for t in range(PACK)]
            for t, sums in enumerate(banks):
                for g in order:
                    first_pass(sums[:], b, g, t, HALF, HALF, g == order[0], g == order[1])
            return banks

        h_codes = {(b, half): sbuf([P, HALF], U32, "h_codes%d%d" % (b, half)) for b, half in ((0, 1), (1, 0), (1, 1))}
        h_codes[0, 0] = placed([P, HALF], U32, "h_codes00", 5 * RAW)
        h_scales = {(b, half): sbuf([P, HALF], U8, "h_scales%d%d" % (b, half)) for b in range(2) for half in range(2)}

        def quantize_h(b, token, rounded):
            half, col = divmod(token, HALF)
            width = rounded.shape[1]
            nc.vector.quantize_mx(
                out=h_codes[b, half][:, col : col + width].bitcast(FP8X4),
                scales=h_scales[b, half][:, col : col + width],
                in_=rounded[:].rearrange("p n t -> p (n t)"),
            )

        def narrow_drain(b, piece, banks):
            rounded = sbuf([P, PIECE, PACK], BF16, "rounded%d%d" % (b, piece))
            for u in range(2):
                nc.vector.tensor_tensor(
                    rounded[:, u * CHUNK : (u + 1) * CHUNK, :],
                    banks[2 * piece + u][:].rearrange("p t n -> p n t"),
                    drift[b][:].to_broadcast([P, CHUNK, PACK]),
                    ALU.add,
                )
            return rounded

        def wide_drain(b, banks, offset):
            tiles = placed([P, PACK, HALF], BF16, "tiles%d" % b, offset)
            for t in range(PACK):
                nc.scalar.activation(tiles[:, t, :], banks[t][:], ACT.Identity, bias=drift[b][:, 0, t : t + 1])
            return tiles

        def interleave(b, token, width, tiles, engine, on=None):
            rounded = sbuf([P, width, PACK], BF16, "woven%d_%d" % (b, token), on)
            col = token - HALF
            dst = rounded[:].rearrange("p (c i) t -> p c t i", i=4)
            src = tiles[:, :, col : col + width].rearrange("p t (c i) -> p c t i", i=4)
            copy_on(engine, dst, src)
            return rounded

        def second_pass(sums, b, c, token, width, start, stop):
            half, col = divmod(token, HALF)
            nc.tensor.matmul_mx(
                out=sums,
                lhsT=c_words[:, b, c * P // 2 : (c + 1) * P // 2].bitcast(FP4X4),
                lhsT_scale=c_scales[:, b, c * P // 4 : (c + 1) * P // 4].bitcast(U8),
                rhs=h_codes[b, half][:, col : col + width].bitcast(FP8X4),
                rhs_scale=h_scales[b, half][:, col : col + width],
                start=start,
                stop=stop,
            )

        def finish(sums, first, token, engine):
            count, width = sums.shape[1], sums.shape[2]
            cost = keep.tile([P, count, width], F32, name="cost%d_%d" % (token, first))
            if engine == "v":
                deviation = keep.tile([P, count, width], F32, name="deviation%d_%d" % (token, first))
                for u in range(count):
                    c = first + u
                    nc.vector.tensor_scalar(
                        deviation[:, u, :], sums[:, u, :], root[:, c : c + 1], shift[:, c : c + 1], ALU.mult, ALU.add
                    )
                nc.vector.tensor_tensor(cost[:], deviation[:], deviation[:], ALU.mult)
            else:
                for u in range(count):
                    c = first + u
                    nc.scalar.activation(
                        cost[:, u, :], sums[:, u, :], ACT.Square, bias=shift[:, c : c + 1], scale=root[:, c : c + 1]
                    )
            rows = out[first * P : (first + count) * P, token : token + width]
            nc.sync.dma_start(rows.rearrange("(u p) n -> p u n", p=P), cost[:])

        def second_product(half, bank0, engines):
            banks = [bank([P, 1, HALF], bank0 + c) for c in range(N // P)]
            for c, sums in enumerate(banks):
                for b in range(2):
                    second_pass(sums[:, 0, :], b, c, half * HALF, HALF, b == 0, b == 1)
            for c, sums in enumerate(banks):
                finish(sums[:], c, half * HALF, engines[c])

        def narrow_second(token, width, plan):
            first = 0
            pending = []
            for number, count, engine in plan:
                sums = bank([P, count, width], number)
                for b in range(2):
                    for u in range(count):
                        start, stop = (b, u) == (0, 0), (b, u) == (1, count - 1)
                        second_pass(sums[:, u, :], b, first + u, token, width, start, stop)
                pending.append((sums, first, count, engine))
                first = first + count
            for sums, first, count, engine in pending:
                step = 1 if width == PIECE else count
                for u in range(0, count, step):
                    finish(sums[:, u : u + step, :], first + u, token, engine)

        narrow0 = narrow_product(0, 0)
        wide0 = wide_product(0, 4, (1, 0))
        rounded0 = [narrow_drain(0, piece, narrow0) for piece in range(2)]
        tiles0 = wide_drain(0, wide0, 4 * RAW)
        narrow1 = narrow_product(1, 0)
        wide1 = wide_product(1, 4, (1, 0))
        for piece in range(2):
            quantize_h(0, piece * PIECE, rounded0[piece])
        turned = keep.tile([P, P], F32, name="turned", align_bytes=64)
        nc.vector.transpose(turned[:], rows)
        nc.scalar.activation(root[:], turned[:, 0:P:32], ACT.Sqrt)
        rounded1 = [narrow_drain(1, piece, narrow1) for piece in range(2)]
        nc.vector.scalar_tensor_tensor(shift[:], turned[:, 1:P:32], -1.0, root[:], ALU.mult, ALU.mult)
        tiles1 = wide_drain(1, wide1, 10 * RAW)
        for piece in range(2):
            quantize_h(1, piece * PIECE, rounded1[piece])
        second_product(0, 0, WIDE)
        for token, width, plan in TAIL:
            early = interleave(0, token, width, tiles0, "v")
            late = interleave(1, token, width, tiles1, "v")
            quantize_h(0, token, early)
            quantize_h(1, token, late)
            narrow_second(token, width, plan)
